import numpy as np
import ml_dtypes


def mxq(x, axis, fmt="e4m3"):
    dtype, down = {"e4m3": (ml_dtypes.float8_e4m3fn, 7), "e5m2": (ml_dtypes.float8_e5m2, 14)}[fmt]
    v = np.moveaxis(np.asarray(x, np.float32).astype(ml_dtypes.bfloat16).astype(np.float64), axis, -1)
    blocks = v.reshape(v.shape[:-1] + (-1, 32))
    amax = np.abs(blocks).max(-1, keepdims=True)
    byte = np.maximum(np.where(amax > 0, np.frexp(amax)[1] - 1 + 127, 0) - down, 1)
    scale = np.exp2(byte - 127.0)
    codes = (blocks / scale).astype(np.float32).astype(dtype).astype(np.float64)
    return np.moveaxis((codes * scale).reshape(v.shape), -1, axis)


WIDE = False


def mx_kscale(k):
    if not WIDE:
        return np.ones(k)
    levels = np.array([10, -10, 5, -5, 0])
    if k % 512:
        return np.exp2(np.random.permutation(np.resize(levels, k // 32))).repeat(32)
    a = np.empty((k // 512, 16))
    for p in range(k // 512):
        a[p, :8] = np.random.permutation(np.resize(levels, 8))
        for g in range(8):
            far = levels[np.abs(levels - a[p, g]) >= 10]
            a[p, g + 8] = far[np.random.randint(len(far))]
    return np.exp2(a.ravel()).repeat(32)


def f64(x):
    return np.asarray(x).astype(np.float64)


def striped(idx):
    return np.tile(np.asarray(idx).reshape(-1, 16).T, (8, 1)).astype(np.uint16)


def unstriped(offs):
    return offs[:16].T.reshape(-1).astype(np.int64)


B, N, T, D, DV, NQ = 1, 1024, 4096, 512, 128, 256


def setup_inputs():
    n = np.random.standard_normal
    idx = np.random.permutation(T)[:B * N]
    s = mx_kscale(D)[:, None]
    u = np.ones(T)
    u[idx] = mx_kscale(B * N)
    r = np.random.uniform(0.5, 2.0, T)
    k = n((D, T)) / s
    v = n((DV, T)) / (u * r)
    return {
        "qT": (n((B, D, NQ)) * s * (1.00 / np.sqrt(D))).astype(np.float32),
        "kT": k.astype(np.float32),
        "vT": v.astype(np.float32),
        "vs": np.tile(u * r, (128, 1)).astype(np.float32),
        "kb": np.tile(n(T), (128, 1)).astype(np.float32),
        "og": n((B, NQ, DV)).astype(np.float32),
        "offs": striped(idx),
    }


def reference(qT, kT, vT, vs, kb, og, offs):
    idx = unstriped(offs)
    k = f64(kT)
    v = f64(vT)
    pick = lambda x: x[:, idx].reshape(x.shape[0], B, N).transpose(1, 0, 2)
    q = f64(qT)
    score = mxq(q, 1, "e4m3").transpose(0, 2, 1) @ mxq(pick(k), 1, "e4m3")
    score = score + pick(f64(kb))[:, :1, :]
    p = score / (1.0 + np.exp(-score))
    w = p * pick(f64(vs))[:, :1, :]
    y = mxq(w, 2, "e4m3") @ mxq(pick(v).transpose(0, 2, 1), 1, "e4m3")
    y = y / 16.0
    y = y / (1.0 + np.exp(-f64(og)))
    return y

@@ -1,0 +1,225 @@
+from contextlib import ExitStack
+
+import concourse.mybir as mybir
+from concourse.masks import make_identity
+
+QUERIES = 256
+FEATURES = 512
+SLOTS = 1024
+TOKENS = 4096
+V_FEATURES = 128
+
+FLOPS = 2 * QUERIES * SLOTS * (FEATURES + V_FEATURES)
+
+F32 = mybir.dt.float32
+BF16 = mybir.dt.bfloat16
+U32 = mybir.dt.uint32
+U16 = mybir.dt.uint16
+U8 = mybir.dt.uint8
+FP8X4 = mybir.dt.float8_e4m3fn_x4
+
+COPY = mybir.ActivationFunctionType.Copy
+SIGMOID = mybir.ActivationFunctionType.Sigmoid
+SILU = mybir.ActivationFunctionType.Silu
+MULT = mybir.AluOpType.mult
+
+P = 128
+PACK = 4
+PASS = P * PACK
+PASSES = SLOTS // PASS
+Q_BLOCKS = QUERIES // P
+
+
+def tile_attend_silu_gate_kernel(tc, qT, kT, vT, vs, kb, og, offs, out):
+    nc = tc.nc
+    with ExitStack() as ctx:
+        keep = ctx.enter_context(tc.tile_pool(name="keep", bufs=1))
+        half = ctx.enter_context(tc.tile_pool(name="half", bufs=2))
+        turn_psum = ctx.enter_context(tc.psum_pool(name="turn_psum", bufs=2))
+        score_psum = ctx.enter_context(tc.psum_pool(name="score_psum", bufs=4))
+        y_psum = ctx.enter_context(tc.psum_pool(name="y_psum", bufs=2))
+
+        offsets = keep.tile([P, SLOTS // 16], U16, name="offsets")
+        ident = keep.tile([P, P], F32, name="ident")
+        kb_row = keep.tile([P, TOKENS], F32, name="kb_row")
+        vs_row = keep.tile([P, TOKENS], F32, name="vs_row")
+        k_planes = [keep.tile([P, TOKENS], F32, name="k_plane%d" % j) for j in range(PACK)]
+        v_pool = keep.tile([P, TOKENS], F32, name="v_pool")
+        q_raw = keep.tile([P, PACK, QUERIES], F32, name="q_raw")
+        gate_in = keep.tile([P, Q_BLOCKS, V_FEATURES], F32, name="gate_in")
+
+        k_rows = kT.rearrange("(p j) n -> j p n", j=PACK)
+
+        share = 3 * TOKENS // 4
+        for row in (kb_row, vs_row):
+            nc.vector.memset(row[:, 0:share], 0.0)
+            nc.gpsimd.memset(row[:, share:TOKENS], 0.0)
+        make_identity(nc, ident[:])
+        nc.scalar.dma_start(gate_in[:], og[0].rearrange("(b p) e -> p b e", p=P))
+        nc.sync.dma_start(offsets[:], offs)
+        nc.sync.dma_start(k_planes[0][:], k_rows[0])
+        nc.sync.dma_start(kb_row[0:1, :], kb[0:1, :])
+        nc.sync.dma_start(k_planes[1][:], k_rows[1])
+        nc.sync.dma_start(vs_row[0:1, :], vs[0:1, :])
+        nc.sync.dma_start(k_planes[2][:], k_rows[2])
+        nc.sync.dma_start(q_raw[:], qT[0].rearrange("(p j) q -> p j q", j=PACK))
+        nc.sync.dma_start(k_planes[3][:], k_rows[3])
+        nc.sync.dma_start(v_pool[:], vT)
+
+        gate = keep.tile([P, Q_BLOCKS, V_FEATURES], F32, name="gate")
+        nc.scalar.activation(gate[:], gate_in[:], SIGMOID)
+        warm = keep.tile([P, 1], F32, name="warm")
+        nc.scalar.activation(warm[:], gate[:, 0, 0:1], SILU)
+
+        k_packed = keep.tile([P, PASSES, PACK, P, PACK], BF16, name="k_packed", align_bytes=64)
+        k_codes = keep.tile([P, SLOTS], U32, name="k_codes", align_bytes=64)
+        k_scales = keep.tile([P, SLOTS], U8, name="k_scales", align_bytes=64)
+
+        k_picked = keep.tile([P, 2, SLOTS], F32, name="k_picked")
+
+        def gather_keys_plain(j):
+            nc.vector.tensor_copy(k_picked[:, j, :], k_planes[j][:].indirect(offsets[:]))
+
+        def interleave_keys(g):
+            nc.scalar.copy(
+                k_packed[:, g, :, :, 0:2],
+                k_picked[:, :, PASS * g : PASS * (g + 1)].rearrange("p j (m t) -> p t m j", t=PACK),
+            )
+
+        def gather_keys(j):
+            nc.vector.tensor_copy(
+                k_packed[:, :, :, :, j].rearrange("p g t m -> p g m t"),
+                k_planes[j][:].indirect(offsets[:]),
+            )
+
+        def gather_keys_half(j, g):
+            nc.vector.tensor_copy(
+                k_packed[:, g, :, :, j].rearrange("p t m -> p m t"),
+                k_planes[j][:].indirect(offsets[:, 32 * g : 32 * g + 32]),
+            )
+
+        def columns(row, name):
+            picked = keep.tile([P, SLOTS], F32, name=name + "_picked")
+            nc.vector.tensor_copy(picked[:], row[:].indirect(offsets[:]))
+            cols = keep.tile([P, PASSES, PACK], F32, name=name + "_cols")
+            for g in range(PASSES):
+                turned = turn_psum.tile([P, PACK, P], F32, name="turned", tag="turned")
+                for t in range(PACK):
+                    nc.tensor.transpose(turned[:, t, :], picked[:, PASS * g + t : PASS * (g + 1) : PACK], ident[:])
+                nc.scalar.copy(cols[:, g, :], turned[:, :, 0])
+            return cols
+
+        gather_keys_plain(0)
+        kb_cols = columns(kb_row, "kb")
+        gather_keys_plain(1)
+        for g in range(PASSES):
+            interleave_keys(g)
+        vs_cols = columns(vs_row, "vs")
+        gather_keys(2)
+        q_packed = keep.tile([P, QUERIES, PACK], BF16, name="q_packed", align_bytes=64)
+        q_codes = keep.tile([P, QUERIES], U32, name="q_codes", align_bytes=64)
+        q_scales = keep.tile([P, QUERIES], U8, name="q_scales", align_bytes=64)
+        nc.scalar.copy(q_packed[:], q_raw[:].rearrange("p j q -> p q j"))
+
+        def quantize_keys(g):
+            cols = slice(PASS * g, PASS * (g + 1))
+            nc.vector.quantize_mx(
+                out=k_codes[:, cols].bitcast(FP8X4),
+                scales=k_scales[:, cols],
+                in_=k_packed[:, g, :, :, :].rearrange("p t m j -> p (t m j)"),
+            )
+
+        p_tiles = [half.tile([P, PACK, QUERIES], F32, name="p_tile%d" % g) for g in range(PASSES)]
+        v_tiles = [half.tile([P, V_FEATURES, PACK], BF16, name="v_packed%d" % g, align_bytes=64) for g in range(PASSES)]
+        w_codes = keep.tile([P, PASSES, QUERIES], U32, name="w_codes", align_bytes=64)
+        w_scales = keep.tile([P, PASSES, QUERIES], U8, name="w_scales", align_bytes=64)
+        v_codes = keep.tile([P, PASSES, V_FEATURES], U32, name="v_codes", align_bytes=64)
+        v_scales = keep.tile([P, PASSES, V_FEATURES], U8, name="v_scales", align_bytes=64)
+
+        def score(g):
+            for pair in range(2):
+                bank = score_psum.tile([P, 2, QUERIES], F32, name="bank")
+                for i in range(2):
+                    c0 = PASS * g + P * (2 * pair + i)
+                    nc.tensor.matmul_mx(
+                        out=bank[:, i, :],
+                        lhsT=k_codes[:, c0 : c0 + P].bitcast(FP8X4),
+                        lhsT_scale=k_scales[:, c0 : c0 + P],
+                        rhs=q_codes[:].bitcast(FP8X4),
+                        rhs_scale=q_scales[:],
+                        start=True,
+                        stop=True,
+                    )
+                for i in range(2):
+                    t = 2 * pair + i
+                    nc.scalar.activation(p_tiles[g][:, t, :], bank[:, i, :], SILU, bias=kb_cols[:, g, t : t + 1])
+
+        w_tiles = []
+
+        def weigh(g):
+            w_packed = half.tile([P, QUERIES, PACK], BF16, name="w_packed", tag="stage", align_bytes=64)
+            w_tiles.append(w_packed)
+            nc.vector.tensor_tensor(
+                w_packed[:],
+                p_tiles[g][:].rearrange("p t q -> p q t"),
+                vs_cols[:, g, :].unsqueeze(1).to_broadcast([P, QUERIES, PACK]),
+                MULT,
+            )
+
+        def quantize_weights(g):
+            nc.vector.quantize_mx(
+                out=w_codes[:, g, :].bitcast(FP8X4),
+                scales=w_scales[:, g, :],
+                in_=w_tiles[g][:].rearrange("p q t -> p (q t)"),
+            )
+
+        def gather_values(g):
+            v_picked = half.tile([P, PASS], F32, name="v_picked", tag="stage", align_bytes=64)
+            nc.vector.tensor_copy(v_picked[:], v_pool[:].indirect(offsets[:, 32 * g : 32 * g + 32]))
+            turned = turn_psum.tile([P, PACK, P], F32, name="turned_v", tag="turned")
+            for t in range(PACK):
+                nc.tensor.transpose(turned[:, t, :], v_picked[:, t:PASS:PACK], ident[:])
+            nc.scalar.copy(v_tiles[g][:], turned[:].rearrange("p t e -> p e t"))
+
+        def quantize_values(g):
+            nc.vector.quantize_mx(
+                out=v_codes[:, g, :].bitcast(FP8X4),
+                scales=v_scales[:, g, :],
+                in_=v_tiles[g][:].rearrange("p e t -> p (e t)"),
+            )
+
+        nc.vector.quantize_mx(
+            out=q_codes[:].bitcast(FP8X4), scales=q_scales[:], in_=q_packed[:].rearrange("p q j -> p (q j)")
+        )
+        gather_keys_half(3, 0)
+        gather_keys_half(3, 1)
+        quantize_keys(0)
+        score(0)
+        quantize_keys(1)
+        score(1)
+        gather_values(0)
+        gather_values(1)
+        weigh(0)
+        weigh(1)
+        quantize_weights(0)
+        quantize_values(0)
+        quantize_values(1)
+        quantize_weights(1)
+
+        for b in range(Q_BLOCKS):
+            q_cols = slice(P * b, P * (b + 1))
+            y = y_psum.tile([P, V_FEATURES], F32, name="y")
+            for g in range(PASSES):
+                nc.tensor.matmul_mx(
+                    out=y[:],
+                    lhsT=w_codes[:, g, q_cols].bitcast(FP8X4),
+                    lhsT_scale=w_scales[:, g, q_cols],
+                    rhs=v_codes[:, g, :].bitcast(FP8X4),
+                    rhs_scale=v_scales[:, g, :],
+                    start=(g == 0),
+                    stop=(g == PASSES - 1),
+                )
+            result = half.tile([P, V_FEATURES], F32, name="result")
+            nc.vector.scalar_tensor_tensor(result[:], y[:], 1.0 / 16.0, gate[:, b, :], MULT, MULT)
+            queue = nc.sync if b == 0 else nc.scalar
+            queue.dma_start(out[0, q_cols, :], result[:])

@@ -28,6 +28,7 @@ PACK = 4
 PASS = P * PACK
 PASSES = SLOTS // PASS
 Q_BLOCKS = QUERIES // P
+RUN = 4
 
 
 def tile_attend_silu_gate_kernel(tc, qT, kT, vT, vs, kb, og, offs, out):
@@ -119,7 +120,10 @@ def tile_attend_silu_gate_kernel(tc, qT, kT, vT, vs, kb, og, offs, out):
         q_packed = keep.tile([P, QUERIES, PACK], BF16, name="q_packed", align_bytes=64)
         q_codes = keep.tile([P, QUERIES], U32, name="q_codes", align_bytes=64)
         q_scales = keep.tile([P, QUERIES], U8, name="q_scales", align_bytes=64)
-        nc.scalar.copy(q_packed[:], q_raw[:].rearrange("p j q -> p q j"))
+        nc.scalar.copy(
+            q_packed[:].rearrange("p (c i) j -> p c j i", i=RUN),
+            q_raw[:].rearrange("p j (c i) -> p c j i", i=RUN),
+        )
 
         def quantize_keys(g):
             cols = slice(PASS * g, PASS * (g + 1))
@@ -160,9 +164,9 @@ def tile_attend_silu_gate_kernel(tc, qT, kT, vT, vs, kb, og, offs, out):
             w_packed = half.tile([P, QUERIES, PACK], BF16, name="w_packed", tag="stage", align_bytes=64)
             w_tiles.append(w_packed)
             nc.vector.tensor_tensor(
-                w_packed[:],
-                p_tiles[g][:].rearrange("p t q -> p q t"),
-                vs_cols[:, g, :].unsqueeze(1).to_broadcast([P, QUERIES, PACK]),
+                w_packed[:].rearrange("p (c i) t -> p c t i", i=RUN),
+                p_tiles[g][:].rearrange("p t (c i) -> p c t i", i=RUN),
+                vs_cols[:, g, :].unsqueeze(1).unsqueeze(3).to_broadcast([P, QUERIES // RUN, PACK, RUN]),
                 MULT,
             )
 
@@ -174,12 +178,16 @@ def tile_attend_silu_gate_kernel(tc, qT, kT, vT, vs, kb, og, offs, out):
             )
 
         def gather_values(g):
-            v_picked = half.tile([P, PASS], F32, name="v_picked", tag="stage", align_bytes=64)
+            v_picked = half.tile([P, PASS], BF16, name="v_picked", tag="stage", align_bytes=64)
             nc.vector.tensor_copy(v_picked[:], v_pool[:].indirect(offsets[:, 32 * g : 32 * g + 32]))
-            turned = turn_psum.tile([P, PACK, P], F32, name="turned_v", tag="turned")
-            for t in range(PACK):
-                nc.tensor.transpose(turned[:, t, :], v_picked[:, t:PASS:PACK], ident[:])
-            nc.scalar.copy(v_tiles[g][:], turned[:].rearrange("p t e -> p e t"))
+            pairs = v_picked[:].bitcast(F32)
+            turned = turn_psum.tile([P, 2, P], F32, name="turned_v", tag="turned")
+            for u in range(2):
+                nc.tensor.transpose(turned[:, u, :], pairs[:, u : PASS // 2 : 2], ident[:])
+            nc.scalar.copy(
+                v_tiles[g][:].rearrange("p e t -> p (e t)").bitcast(F32).rearrange("p (e u) -> p e u", u=2),
+                turned[:].rearrange("p u e -> p e u"),
+            )
 
         def quantize_values(g):
             nc.vector.quantize_mx(

@@ -22,6 +22,7 @@ COPY = mybir.ActivationFunctionType.Copy
 SIGMOID = mybir.ActivationFunctionType.Sigmoid
 SILU = mybir.ActivationFunctionType.Silu
 MULT = mybir.AluOpType.mult
+ADD = mybir.AluOpType.add
 
 P = 128
 PACK = 4
@@ -29,6 +30,10 @@ PASS = P * PACK
 PASSES = SLOTS // PASS
 Q_BLOCKS = QUERIES // P
 RUN = 4
+PIECES = 2
+PIECE_STEP = 64
+KB_PART = 0
+VS_PART = 4
 
 
 def tile_attend_silu_gate_kernel(tc, qT, kT, vT, vs, kb, og, offs, out):
@@ -57,11 +62,18 @@ def tile_attend_silu_gate_kernel(tc, qT, kT, vT, vs, kb, og, offs, out):
             nc.gpsimd.memset(row[:, share:TOKENS], 0.0)
         make_identity(nc, ident[:])
         nc.scalar.dma_start(gate_in[:], og[0].rearrange("(b p) e -> p b e", p=P))
-        nc.sync.dma_start(offsets[:], offs)
+
+        def load_row(row, source, first):
+            for piece in range(PIECES):
+                part = first + piece * PIECE_STEP
+                tokens = slice(piece * TOKENS // PIECES, (piece + 1) * TOKENS // PIECES)
+                nc.sync.dma_start(row[part : part + 1, tokens], source[part : part + 1, tokens])
+
         nc.sync.dma_start(k_planes[0][:], k_rows[0])
-        nc.sync.dma_start(kb_row[0:1, :], kb[0:1, :])
+        nc.sync.dma_start(offsets[:], offs)
+        load_row(kb_row, kb, KB_PART)
         nc.sync.dma_start(k_planes[1][:], k_rows[1])
-        nc.sync.dma_start(vs_row[0:1, :], vs[0:1, :])
+        load_row(vs_row, vs, VS_PART)
         nc.sync.dma_start(k_planes[2][:], k_rows[2])
         nc.sync.dma_start(q_raw[:], qT[0].rearrange("(p j) q -> p j q", j=PACK))
         nc.sync.dma_start(k_planes[3][:], k_rows[3])
@@ -99,23 +111,25 @@ def tile_attend_silu_gate_kernel(tc, qT, kT, vT, vs, kb, og, offs, out):
                 k_planes[j][:].indirect(offsets[:, 32 * g : 32 * g + 32]),
             )
 
-        def columns(row, name):
+        def columns(row, first, name):
             picked = keep.tile([P, SLOTS], F32, name=name + "_picked")
             nc.vector.tensor_copy(picked[:], row[:].indirect(offsets[:]))
+            parts = keep.tile([P, PASSES, PACK, PIECES], F32, name=name + "_parts")
             cols = keep.tile([P, PASSES, PACK], F32, name=name + "_cols")
             for g in range(PASSES):
                 turned = turn_psum.tile([P, PACK, P], F32, name="turned", tag="turned")
                 for t in range(PACK):
                     nc.tensor.transpose(turned[:, t, :], picked[:, PASS * g + t : PASS * (g + 1) : PACK], ident[:])
-                nc.scalar.copy(cols[:, g, :], turned[:, :, 0])
+                nc.scalar.copy(parts[:, g, :, :], turned[:, :, first:P:PIECE_STEP])
+            nc.gpsimd.tensor_tensor(cols[:], parts[:, :, :, 0], parts[:, :, :, 1], ADD)
             return cols
 
         gather_keys_plain(0)
-        kb_cols = columns(kb_row, "kb")
+        kb_cols = columns(kb_row, KB_PART, "kb")
         gather_keys_plain(1)
         for g in range(PASSES):
             interleave_keys(g)
-        vs_cols = columns(vs_row, "vs")
+        vs_cols = columns(vs_row, VS_PART, "vs")
         gather_keys(2)
         q_packed = keep.tile([P, QUERIES, PACK], BF16, name="q_packed", align_bytes=64)
         q_codes = keep.tile([P, QUERIES], U32, name="q_codes", align_bytes=64)

@@ -75,8 +75,8 @@ def tile_attend_silu_gate_kernel(tc, qT, kT, vT, vs, kb, og, offs, out):
         nc.sync.dma_start(k_planes[1][:], k_rows[1])
         load_row(vs_row, vs, VS_PART)
         nc.sync.dma_start(k_planes[2][:], k_rows[2])
-        nc.sync.dma_start(q_raw[:], qT[0].rearrange("(p j) q -> p j q", j=PACK))
         nc.sync.dma_start(k_planes[3][:], k_rows[3])
+        nc.sync.dma_start(q_raw[:], qT[0].rearrange("(p j) q -> p j q", j=PACK))
         nc.sync.dma_start(v_pool[:], vT)
 
         gate = keep.tile([P, Q_BLOCKS, V_FEATURES], F32, name="gate")
@@ -85,7 +85,6 @@ def tile_attend_silu_gate_kernel(tc, qT, kT, vT, vs, kb, og, offs, out):
         nc.scalar.activation(warm[:], gate[:, 0, 0:1], SILU)
 
         k_packed = keep.tile([P, PASSES, PACK, P, PACK], BF16, name="k_packed", align_bytes=64)
-        k_codes = keep.tile([P, SLOTS], U32, name="k_codes", align_bytes=64)
         k_scales = keep.tile([P, SLOTS], U8, name="k_scales", align_bytes=64)
 
         k_picked = keep.tile([P, 2, SLOTS], F32, name="k_picked")
@@ -131,7 +130,7 @@ def tile_attend_silu_gate_kernel(tc, qT, kT, vT, vs, kb, og, offs, out):
             interleave_keys(g)
         vs_cols = columns(vs_row, VS_PART, "vs")
         gather_keys(2)
-        q_packed = keep.tile([P, QUERIES, PACK], BF16, name="q_packed", align_bytes=64)
+        q_packed = keep.tile([P, QUERIES, PACK], BF16, name="q_packed", tag="q_then_k", align_bytes=64)
         q_codes = keep.tile([P, QUERIES], U32, name="q_codes", align_bytes=64)
         q_scales = keep.tile([P, QUERIES], U8, name="q_scales", align_bytes=64)
         nc.scalar.copy(
@@ -139,17 +138,21 @@ def tile_attend_silu_gate_kernel(tc, qT, kT, vT, vs, kb, og, offs, out):
             q_raw[:].rearrange("p j (c i) -> p c j i", i=RUN),
         )
 
+        k_codes = []
+
         def quantize_keys(g):
             cols = slice(PASS * g, PASS * (g + 1))
+            tag = "q_then_k" if g == PASSES - 1 else "k_codes"
+            k_codes.append(keep.tile([P, PASS], U32, name="k_codes%d" % g, tag=tag, align_bytes=64))
             nc.vector.quantize_mx(
-                out=k_codes[:, cols].bitcast(FP8X4),
+                out=k_codes[g][:].bitcast(FP8X4),
                 scales=k_scales[:, cols],
                 in_=k_packed[:, g, :, :, :].rearrange("p t m j -> p (t m j)"),
             )
 
         p_tiles = [half.tile([P, PACK, QUERIES], F32, name="p_tile%d" % g) for g in range(PASSES)]
         v_tiles = [half.tile([P, V_FEATURES, PACK], BF16, name="v_packed%d" % g, align_bytes=64) for g in range(PASSES)]
-        w_codes = keep.tile([P, PASSES, QUERIES], U32, name="w_codes", align_bytes=64)
+        w_codes = []
         w_scales = keep.tile([P, PASSES, QUERIES], U8, name="w_scales", align_bytes=64)
         v_codes = keep.tile([P, PASSES, V_FEATURES], U32, name="v_codes", align_bytes=64)
         v_scales = keep.tile([P, PASSES, V_FEATURES], U8, name="v_scales", align_bytes=64)
@@ -158,11 +161,11 @@ def tile_attend_silu_gate_kernel(tc, qT, kT, vT, vs, kb, og, offs, out):
             for pair in range(2):
                 bank = score_psum.tile([P, 2, QUERIES], F32, name="bank")
                 for i in range(2):
-                    c0 = PASS * g + P * (2 * pair + i)
+                    c0 = P * (2 * pair + i)
                     nc.tensor.matmul_mx(
                         out=bank[:, i, :],
-                        lhsT=k_codes[:, c0 : c0 + P].bitcast(FP8X4),
-                        lhsT_scale=k_scales[:, c0 : c0 + P],
+                        lhsT=k_codes[g][:, c0 : c0 + P].bitcast(FP8X4),
+                        lhsT_scale=k_scales[:, PASS * g + c0 : PASS * g + c0 + P],
                         rhs=q_codes[:].bitcast(FP8X4),
                         rhs_scale=q_scales[:],
                         start=True,
@@ -175,9 +178,11 @@ def tile_attend_silu_gate_kernel(tc, qT, kT, vT, vs, kb, og, offs, out):
         w_tiles = []
 
         def weigh(g):
-            w_packed = half.tile([P, QUERIES, PACK], BF16, name="w_packed", tag="stage", align_bytes=64)
+            tag = "stage" if g == PASSES - 1 else "w_first"
+            w_packed = half.tile([P, QUERIES, PACK], BF16, name="w_packed", tag=tag, align_bytes=64)
             w_tiles.append(w_packed)
-            nc.vector.tensor_tensor(
+            engine = nc.vector if g == PASSES - 1 else nc.gpsimd
+            engine.tensor_tensor(
                 w_packed[:].rearrange("p (c i) t -> p c t i", i=RUN),
                 p_tiles[g][:].rearrange("p t (c i) -> p c t i", i=RUN),
                 vs_cols[:, g, :].unsqueeze(1).unsqueeze(3).to_broadcast([P, QUERIES // RUN, PACK, RUN]),
@@ -185,8 +190,10 @@ def tile_attend_silu_gate_kernel(tc, qT, kT, vT, vs, kb, og, offs, out):
             )
 
         def quantize_weights(g):
+            tag = "stage" if g == 0 else "w_codes"
+            w_codes.append(half.tile([P, QUERIES], U32, name="w_codes%d" % g, tag=tag, align_bytes=64))
             nc.vector.quantize_mx(
-                out=w_codes[:, g, :].bitcast(FP8X4),
+                out=w_codes[g][:].bitcast(FP8X4),
                 scales=w_scales[:, g, :],
                 in_=w_tiles[g][:].rearrange("p q t -> p (q t)"),
             )
@@ -210,12 +217,12 @@ def tile_attend_silu_gate_kernel(tc, qT, kT, vT, vs, kb, og, offs, out):
                 in_=v_tiles[g][:].rearrange("p e t -> p (e t)"),
             )
 
-        nc.vector.quantize_mx(
-            out=q_codes[:].bitcast(FP8X4), scales=q_scales[:], in_=q_packed[:].rearrange("p q j -> p (q j)")
-        )
         gather_keys_half(3, 0)
         gather_keys_half(3, 1)
         quantize_keys(0)
+        nc.vector.quantize_mx(
+            out=q_codes[:].bitcast(FP8X4), scales=q_scales[:], in_=q_packed[:].rearrange("p q j -> p (q j)")
+        )
         score(0)
         quantize_keys(1)
         score(1)
@@ -234,7 +241,7 @@ def tile_attend_silu_gate_kernel(tc, qT, kT, vT, vs, kb, og, offs, out):
             for g in range(PASSES):
                 nc.tensor.matmul_mx(
                     out=y[:],
-                    lhsT=w_codes[:, g, q_cols].bitcast(FP8X4),
+                    lhsT=w_codes[g][:, q_cols].bitcast(FP8X4),
                     lhsT_scale=w_scales[:, g, q_cols],
                     rhs=v_codes[:, g, :].bitcast(FP8X4),
                     rhs_scale=v_scales[:, g, :],

@@ -178,15 +178,26 @@ def tile_attend_silu_gate_kernel(tc, qT, kT, vT, vs, kb, og, offs, out):
         w_tiles = []
 
         def weigh(g):
-            tag = "stage" if g == PASSES - 1 else "w_first"
-            w_packed = half.tile([P, QUERIES, PACK], BF16, name="w_packed", tag=tag, align_bytes=64)
+            w_packed = half.tile([P, QUERIES, PACK], BF16, name="w_packed", tag="stage", align_bytes=64)
             w_tiles.append(w_packed)
-            engine = nc.vector if g == PASSES - 1 else nc.gpsimd
-            engine.tensor_tensor(
+            nc.vector.tensor_tensor(
                 w_packed[:].rearrange("p (c i) t -> p c t i", i=RUN),
                 p_tiles[g][:].rearrange("p t (c i) -> p c t i", i=RUN),
                 vs_cols[:, g, :].unsqueeze(1).unsqueeze(3).to_broadcast([P, QUERIES // RUN, PACK, RUN]),
                 MULT,
+            )
+
+        def weigh_in_pairs(g):
+            pairs = keep.tile([P, 2, QUERIES, 2], BF16, name="w_pairs")
+            for t in range(PACK):
+                nc.gpsimd.tensor_scalar(
+                    pairs[:, t // 2, :, t % 2], p_tiles[g][:, t, :], vs_cols[:, g, t : t + 1], 0.0, MULT, ADD
+                )
+            w_packed = keep.tile([P, QUERIES, PACK], BF16, name="w_first", align_bytes=64)
+            w_tiles.append(w_packed)
+            nc.scalar.copy(
+                w_packed[:].rearrange("p q t -> p (q t)").bitcast(F32).rearrange("p (q u) -> p q u", u=2),
+                pairs[:].rearrange("p u q e -> p u (q e)").bitcast(F32).rearrange("p u q -> p q u"),
             )
 
         def quantize_weights(g):
@@ -228,7 +239,7 @@ def tile_attend_silu_gate_kernel(tc, qT, kT, vT, vs, kb, og, offs, out):
         score(1)
         gather_values(0)
         gather_values(1)
-        weigh(0)
+        weigh_in_pairs(0)
         weigh(1)
         quantize_weights(0)
         quantize_values(0)

@@ -129,6 +129,15 @@ def tile_attend_silu_gate_kernel(tc, qT, kT, vT, vs, kb, og, offs, out):
         for g in range(PASSES):
             interleave_keys(g)
         vs_cols = columns(vs_row, VS_PART, "vs")
+        vs_wide = keep.tile([P, P], F32, name="vs_wide")
+        nc.gpsimd.memset(vs_wide[:, PACK:P], 0.0)
+        nc.gpsimd.tensor_copy(vs_wide[:, 0:PACK], vs_cols[:, PASSES - 1, :])
+        vs_there = turn_psum.tile([P, P], F32, name="vs_there", tag="turned")
+        nc.tensor.transpose(vs_there[:], vs_wide[:], ident[:])
+        vs_turned = keep.tile([P, P], F32, name="vs_turned")
+        nc.scalar.copy(vs_turned[:], vs_there[:])
+        vs_back = y_psum.tile([P, P], F32, name="vs_back", tag="y")
+        nc.tensor.transpose(vs_back[:], vs_turned[:], ident[:])
         gather_keys(2)
         q_packed = keep.tile([P, QUERIES, PACK], BF16, name="q_packed", tag="q_then_k", align_bytes=64)
         q_codes = keep.tile([P, QUERIES], U32, name="q_codes", align_bytes=64)
@@ -183,7 +192,7 @@ def tile_attend_silu_gate_kernel(tc, qT, kT, vT, vs, kb, og, offs, out):
             nc.vector.tensor_tensor(
                 w_packed[:].rearrange("p (c i) t -> p c t i", i=RUN),
                 p_tiles[g][:].rearrange("p t (c i) -> p c t i", i=RUN),
-                vs_cols[:, g, :].unsqueeze(1).unsqueeze(3).to_broadcast([P, QUERIES // RUN, PACK, RUN]),
+                vs_back[:, 0:PACK].unsqueeze(1).unsqueeze(3).to_broadcast([P, QUERIES // RUN, PACK, RUN]),
                 MULT,
             )
 
@@ -248,7 +257,7 @@ def tile_attend_silu_gate_kernel(tc, qT, kT, vT, vs, kb, og, offs, out):
 
         for b in range(Q_BLOCKS):
             q_cols = slice(P * b, P * (b + 1))
-            y = y_psum.tile([P, V_FEATURES], F32, name="y")
+            y = y_psum.tile([P, V_FEATURES], F32, name="y", tag="y")
             for g in range(PASSES):
                 nc.tensor.matmul_mx(
                     out=y[:],

@@ -34,6 +34,7 @@ PIECES = 2
 PIECE_STEP = 64
 KB_PART = 0
 VS_PART = 4
+SHARE = 96
 
 
 def tile_attend_silu_gate_kernel(tc, qT, kT, vT, vs, kb, og, offs, out):
@@ -84,7 +85,10 @@ def tile_attend_silu_gate_kernel(tc, qT, kT, vT, vs, kb, og, offs, out):
         warm = keep.tile([P, 1], F32, name="warm")
         nc.scalar.activation(warm[:], gate[:, 0, 0:1], SILU)
 
-        k_packed = keep.tile([P, PASSES, PACK, P, PACK], BF16, name="k_packed", align_bytes=64)
+        k_packed = [
+            keep.tile([P, PACK, P, PACK], BF16, name="k_packed%d" % g, tag="k_stage%d" % g, align_bytes=64)
+            for g in range(PASSES)
+        ]
         k_scales = keep.tile([P, SLOTS], U8, name="k_scales", align_bytes=64)
 
         k_picked = keep.tile([P, 2, SLOTS], F32, name="k_picked")
@@ -94,19 +98,13 @@ def tile_attend_silu_gate_kernel(tc, qT, kT, vT, vs, kb, og, offs, out):
 
         def interleave_keys(g):
             nc.scalar.copy(
-                k_packed[:, g, :, :, 0:2],
+                k_packed[g][:, :, :, 0:2],
                 k_picked[:, :, PASS * g : PASS * (g + 1)].rearrange("p j (m t) -> p t m j", t=PACK),
-            )
-
-        def gather_keys(j):
-            nc.vector.tensor_copy(
-                k_packed[:, :, :, :, j].rearrange("p g t m -> p g m t"),
-                k_planes[j][:].indirect(offsets[:]),
             )
 
         def gather_keys_half(j, g):
             nc.vector.tensor_copy(
-                k_packed[:, g, :, :, j].rearrange("p t m -> p m t"),
+                k_packed[g][:, :, :, j].rearrange("p t m -> p m t"),
                 k_planes[j][:].indirect(offsets[:, 32 * g : 32 * g + 32]),
             )
 
@@ -138,7 +136,8 @@ def tile_attend_silu_gate_kernel(tc, qT, kT, vT, vs, kb, og, offs, out):
         nc.scalar.copy(vs_turned[:], vs_there[:])
         vs_back = y_psum.tile([P, P], F32, name="vs_back", tag="y")
         nc.tensor.transpose(vs_back[:], vs_turned[:], ident[:])
-        gather_keys(2)
+        gather_keys_half(2, 0)
+        gather_keys_half(2, 1)
         q_packed = keep.tile([P, QUERIES, PACK], BF16, name="q_packed", tag="q_then_k", align_bytes=64)
         q_codes = keep.tile([P, QUERIES], U32, name="q_codes", align_bytes=64)
         q_scales = keep.tile([P, QUERIES], U8, name="q_scales", align_bytes=64)
@@ -147,52 +146,57 @@ def tile_attend_silu_gate_kernel(tc, qT, kT, vT, vs, kb, og, offs, out):
             q_raw[:].rearrange("p j (c i) -> p c j i", i=RUN),
         )
 
-        k_codes = []
+        k_codes = {}
 
-        def quantize_keys(g):
-            cols = slice(PASS * g, PASS * (g + 1))
-            tag = "q_then_k" if g == PASSES - 1 else "k_codes"
-            k_codes.append(keep.tile([P, PASS], U32, name="k_codes%d" % g, tag=tag, align_bytes=64))
+        def quantize_keys(g, t0, t1, tag):
+            codes = keep.tile([P, P * (t1 - t0)], U32, name="k_codes%d_%d" % (g, t0), tag=tag, align_bytes=64)
+            for t in range(t0, t1):
+                k_codes[g, t] = codes[:, P * (t - t0) : P * (t - t0 + 1)]
             nc.vector.quantize_mx(
-                out=k_codes[g][:].bitcast(FP8X4),
-                scales=k_scales[:, cols],
-                in_=k_packed[:, g, :, :, :].rearrange("p t m j -> p (t m j)"),
+                out=codes[:].bitcast(FP8X4),
+                scales=k_scales[:, PASS * g + P * t0 : PASS * g + P * t1],
+                in_=k_packed[g][:, t0:t1, :, :].rearrange("p t m j -> p (t m j)"),
             )
 
-        p_tiles = [half.tile([P, PACK, QUERIES], F32, name="p_tile%d" % g) for g in range(PASSES)]
+        p_tiles = [keep.tile([P, PACK, QUERIES], F32, name="p_tile%d" % g, tag="p%d" % g, align_bytes=64) for g in range(PASSES)]
+        w_second = keep.tile([P, QUERIES * PACK], BF16, name="w_second", align_bytes=64)
+        v_second = keep.tile([P, PASS], BF16, name="v_second", align_bytes=64)
         v_tiles = [half.tile([P, V_FEATURES, PACK], BF16, name="v_packed%d" % g, align_bytes=64) for g in range(PASSES)]
         w_codes = []
         w_scales = keep.tile([P, PASSES, QUERIES], U8, name="w_scales", align_bytes=64)
-        v_codes = keep.tile([P, PASSES, V_FEATURES], U32, name="v_codes", align_bytes=64)
+        v_codes = []
         v_scales = keep.tile([P, PASSES, V_FEATURES], U8, name="v_scales", align_bytes=64)
 
         def score(g):
-            for pair in range(2):
-                bank = score_psum.tile([P, 2, QUERIES], F32, name="bank")
-                for i in range(2):
-                    c0 = P * (2 * pair + i)
-                    nc.tensor.matmul_mx(
-                        out=bank[:, i, :],
-                        lhsT=k_codes[g][:, c0 : c0 + P].bitcast(FP8X4),
-                        lhsT_scale=k_scales[:, PASS * g + c0 : PASS * g + c0 + P],
-                        rhs=q_codes[:].bitcast(FP8X4),
-                        rhs_scale=q_scales[:],
-                        start=True,
-                        stop=True,
-                    )
-                for i in range(2):
-                    t = 2 * pair + i
-                    nc.scalar.activation(p_tiles[g][:, t, :], bank[:, i, :], SILU, bias=kb_cols[:, g, t : t + 1])
+            for t in range(PACK):
+                bank = score_psum.tile([P, QUERIES], F32, name="bank")
+                nc.tensor.matmul_mx(
+                    out=bank[:],
+                    lhsT=k_codes[g, t].bitcast(FP8X4),
+                    lhsT_scale=k_scales[:, PASS * g + P * t : PASS * g + P * (t + 1)],
+                    rhs=q_codes[:].bitcast(FP8X4),
+                    rhs_scale=q_scales[:],
+                    start=True,
+                    stop=True,
+                )
+                nc.scalar.activation(p_tiles[g][:, t, :], bank[:], SILU, bias=kb_cols[:, g, t : t + 1])
 
         w_tiles = []
 
         def weigh(g):
-            w_packed = half.tile([P, QUERIES, PACK], BF16, name="w_packed", tag="stage", align_bytes=64)
+            w_packed = w_second[:].rearrange("p (q t) -> p q t", t=PACK)
             w_tiles.append(w_packed)
+            own = QUERIES - SHARE
             nc.vector.tensor_tensor(
-                w_packed[:].rearrange("p (c i) t -> p c t i", i=RUN),
-                p_tiles[g][:].rearrange("p t (c i) -> p c t i", i=RUN),
-                vs_back[:, 0:PACK].unsqueeze(1).unsqueeze(3).to_broadcast([P, QUERIES // RUN, PACK, RUN]),
+                w_packed[:, 0:own, :].rearrange("p (c i) t -> p c t i", i=RUN),
+                p_tiles[g][:, :, 0:own].rearrange("p t (c i) -> p c t i", i=RUN),
+                vs_back[:, 0:PACK].unsqueeze(1).unsqueeze(3).to_broadcast([P, own // RUN, PACK, RUN]),
+                MULT,
+            )
+            nc.gpsimd.tensor_tensor(
+                w_packed[:, own:QUERIES, :].rearrange("p (c i) t -> p c t i", i=RUN),
+                p_tiles[g][:, :, own:QUERIES].rearrange("p t (c i) -> p c t i", i=RUN),
+                vs_cols[:, g, :].unsqueeze(1).unsqueeze(3).to_broadcast([P, SHARE // RUN, PACK, RUN]),
                 MULT,
             )
 
@@ -202,26 +206,27 @@ def tile_attend_silu_gate_kernel(tc, qT, kT, vT, vs, kb, og, offs, out):
                 nc.gpsimd.tensor_scalar(
                     pairs[:, t // 2, :, t % 2], p_tiles[g][:, t, :], vs_cols[:, g, t : t + 1], 0.0, MULT, ADD
                 )
-            w_packed = keep.tile([P, QUERIES, PACK], BF16, name="w_first", align_bytes=64)
+            w_packed = keep.tile([P, QUERIES, PACK], BF16, name="w_first", tag="w_then_v", align_bytes=64)
             w_tiles.append(w_packed)
             nc.scalar.copy(
                 w_packed[:].rearrange("p q t -> p (q t)").bitcast(F32).rearrange("p (q u) -> p q u", u=2),
                 pairs[:].rearrange("p u q e -> p u (q e)").bitcast(F32).rearrange("p u q -> p q u"),
             )
 
-        def quantize_weights(g):
-            tag = "stage" if g == 0 else "w_codes"
-            w_codes.append(half.tile([P, QUERIES], U32, name="w_codes%d" % g, tag=tag, align_bytes=64))
+        def quantize_weights(g, q_cols):
+            if len(w_codes) == g:
+                tag = "p1" if g == 0 else "w_codes"
+                w_codes.append(keep.tile([P, QUERIES], U32, name="w_codes%d" % g, tag=tag, align_bytes=64))
             nc.vector.quantize_mx(
-                out=w_codes[g][:].bitcast(FP8X4),
-                scales=w_scales[:, g, :],
-                in_=w_tiles[g][:].rearrange("p q t -> p (q t)"),
+                out=w_codes[g][:, q_cols].bitcast(FP8X4),
+                scales=w_scales[:, g, q_cols],
+                in_=w_tiles[g][:, q_cols, :].rearrange("p q t -> p (q t)"),
             )
 
         def gather_values(g):
-            v_picked = half.tile([P, PASS], BF16, name="v_picked", tag="stage", align_bytes=64)
-            nc.vector.tensor_copy(v_picked[:], v_pool[:].indirect(offsets[:, 32 * g : 32 * g + 32]))
-            pairs = v_picked[:].bitcast(F32)
+            v_picked = w_second[:, 0:PASS] if g == 0 else v_second[:]
+            nc.vector.tensor_copy(v_picked, v_pool[:].indirect(offsets[:, 32 * g : 32 * g + 32]))
+            pairs = v_picked.bitcast(F32)
             turned = turn_psum.tile([P, 2, P], F32, name="turned_v", tag="turned")
             for u in range(2):
                 nc.tensor.transpose(turned[:, u, :], pairs[:, u : PASS // 2 : 2], ident[:])
@@ -231,29 +236,32 @@ def tile_attend_silu_gate_kernel(tc, qT, kT, vT, vs, kb, og, offs, out):
             )
 
         def quantize_values(g):
+            tag = "v_codes" if g == 0 else "w_then_v"
+            v_codes.append(keep.tile([P, V_FEATURES], U32, name="v_codes%d" % g, tag=tag, align_bytes=64))
             nc.vector.quantize_mx(
-                out=v_codes[:, g, :].bitcast(FP8X4),
+                out=v_codes[g][:].bitcast(FP8X4),
                 scales=v_scales[:, g, :],
                 in_=v_tiles[g][:].rearrange("p e t -> p (e t)"),
             )
 
         gather_keys_half(3, 0)
         gather_keys_half(3, 1)
-        quantize_keys(0)
+        quantize_keys(0, 0, 2, "k_first")
         nc.vector.quantize_mx(
             out=q_codes[:].bitcast(FP8X4), scales=q_scales[:], in_=q_packed[:].rearrange("p q j -> p (q j)")
         )
+        quantize_keys(0, 2, 4, "q_then_k")
         score(0)
-        quantize_keys(1)
+        quantize_keys(1, 0, 4, "k_stage0")
         score(1)
         gather_values(0)
         gather_values(1)
         weigh_in_pairs(0)
         weigh(1)
-        quantize_weights(0)
+        quantize_weights(0, slice(0, QUERIES))
         quantize_values(0)
+        quantize_weights(1, slice(0, QUERIES))
         quantize_values(1)
-        quantize_weights(1)
 
         for b in range(Q_BLOCKS):
             q_cols = slice(P * b, P * (b + 1))
@@ -263,7 +271,7 @@ def tile_attend_silu_gate_kernel(tc, qT, kT, vT, vs, kb, og, offs, out):
                     out=y[:],
                     lhsT=w_codes[g][:, q_cols].bitcast(FP8X4),
                     lhsT_scale=w_scales[:, g, q_cols],
-                    rhs=v_codes[:, g, :].bitcast(FP8X4),
+                    rhs=v_codes[g][:].bitcast(FP8X4),
                     rhs_scale=v_scales[:, g, :],
                     start=(g == 0),
                     stop=(g == PASSES - 1),

@@ -62,7 +62,7 @@ def tile_attend_silu_gate_kernel(tc, qT, kT, vT, vs, kb, og, offs, out):
             nc.vector.memset(row[:, 0:share], 0.0)
             nc.gpsimd.memset(row[:, share:TOKENS], 0.0)
         make_identity(nc, ident[:])
-        nc.scalar.dma_start(gate_in[:], og[0].rearrange("(b p) e -> p b e", p=P))
+        nc.scalar.dma_start(gate_in[:], og[0].rearrange("(p b) e -> p b e", b=Q_BLOCKS))
 
         def load_row(row, source, first):
             for piece in range(PIECES):
@@ -142,8 +142,8 @@ def tile_attend_silu_gate_kernel(tc, qT, kT, vT, vs, kb, og, offs, out):
         q_codes = keep.tile([P, QUERIES], U32, name="q_codes", align_bytes=64)
         q_scales = keep.tile([P, QUERIES], U8, name="q_scales", align_bytes=64)
         nc.scalar.copy(
-            q_packed[:].rearrange("p (c i) j -> p c j i", i=RUN),
-            q_raw[:].rearrange("p j (c i) -> p c j i", i=RUN),
+            q_packed[:].rearrange("p (b c i) j -> p c j i b", b=Q_BLOCKS, i=RUN // Q_BLOCKS),
+            q_raw[:].rearrange("p j (c i b) -> p c j i b", b=Q_BLOCKS, i=RUN // Q_BLOCKS),
         )
 
         k_codes = {}
@@ -260,8 +260,9 @@ def tile_attend_silu_gate_kernel(tc, qT, kT, vT, vs, kb, og, offs, out):
         weigh(1)
         quantize_weights(0, slice(0, QUERIES))
         quantize_values(0)
-        quantize_weights(1, slice(0, QUERIES))
+        quantize_weights(1, slice(0, P))
         quantize_values(1)
+        quantize_weights(1, slice(P, QUERIES))
 
         for b in range(Q_BLOCKS):
             q_cols = slice(P * b, P * (b + 1))
@@ -278,5 +279,5 @@ def tile_attend_silu_gate_kernel(tc, qT, kT, vT, vs, kb, og, offs, out):
                 )
             result = half.tile([P, V_FEATURES], F32, name="result")
             nc.vector.scalar_tensor_tensor(result[:], y[:], 1.0 / 16.0, gate[:, b, :], MULT, MULT)
-            queue = nc.sync if b == 0 else nc.scalar
-            queue.dma_start(out[0, q_cols, :], result[:])
+            queue = nc.scalar if b == 0 else nc.sync
+            queue.dma_start(out[0].rearrange("(p b) e -> b p e", b=Q_BLOCKS)[b], result[:])

@@ -225,11 +225,14 @@ def tile_attend_silu_gate_kernel(tc, qT, kT, vT, vs, kb, og, offs, out):
 
         def gather_values(g):
             v_picked = w_second[:, 0:PASS] if g == 0 else v_second[:]
-            nc.vector.tensor_copy(v_picked, v_pool[:].indirect(offsets[:, 32 * g : 32 * g + 32]))
+            nc.vector.tensor_copy(
+                v_picked.rearrange("p (u m e) -> p m u e", u=2, e=2),
+                v_pool[:].indirect(offsets[:, 32 * g : 32 * g + 32]),
+            )
             pairs = v_picked.bitcast(F32)
             turned = turn_psum.tile([P, 2, P], F32, name="turned_v", tag="turned")
             for u in range(2):
-                nc.tensor.transpose(turned[:, u, :], pairs[:, u : PASS // 2 : 2], ident[:])
+                nc.tensor.transpose(turned[:, u, :], pairs[:, P * u : P * (u + 1)], ident[:])
             nc.scalar.copy(
                 v_tiles[g][:].rearrange("p e t -> p (e t)").bitcast(F32).rearrange("p (e u) -> p e u", u=2),
                 turned[:].rearrange("p u e -> p e u"),

@@ -34,7 +34,7 @@ PIECES = 2
 PIECE_STEP = 64
 KB_PART = 0
 VS_PART = 4
-SHARE = 96
+SHARE = 80
 
 
 def tile_attend_silu_gate_kernel(tc, qT, kT, vT, vs, kb, og, offs, out):
@@ -42,6 +42,7 @@ def tile_attend_silu_gate_kernel(tc, qT, kT, vT, vs, kb, og, offs, out):
     with ExitStack() as ctx:
         keep = ctx.enter_context(tc.tile_pool(name="keep", bufs=1))
         half = ctx.enter_context(tc.tile_pool(name="half", bufs=2))
+        tail = ctx.enter_context(tc.tile_pool(name="tail", bufs=1))
         turn_psum = ctx.enter_context(tc.psum_pool(name="turn_psum", bufs=2))
         score_psum = ctx.enter_context(tc.psum_pool(name="score_psum", bufs=4))
         y_psum = ctx.enter_context(tc.psum_pool(name="y_psum", bufs=2))
@@ -159,7 +160,7 @@ def tile_attend_silu_gate_kernel(tc, qT, kT, vT, vs, kb, og, offs, out):
             )
 
         p_tiles = [keep.tile([P, PACK, QUERIES], F32, name="p_tile%d" % g, tag="p%d" % g, align_bytes=64) for g in range(PASSES)]
-        w_second = keep.tile([P, QUERIES * PACK], BF16, name="w_second", align_bytes=64)
+        v_first = tail.tile([P, PASS], BF16, name="v_first", align_bytes=64, offset=1536)
         v_second = keep.tile([P, PASS], BF16, name="v_second", align_bytes=64)
         v_tiles = [half.tile([P, V_FEATURES, PACK], BF16, name="v_packed%d" % g, align_bytes=64) for g in range(PASSES)]
         w_codes = []
@@ -184,7 +185,7 @@ def tile_attend_silu_gate_kernel(tc, qT, kT, vT, vs, kb, og, offs, out):
         w_tiles = []
 
         def weigh(g):
-            w_packed = w_second[:].rearrange("p (q t) -> p q t", t=PACK)
+            w_packed = tail.tile([P, QUERIES, PACK], BF16, name="w_second", align_bytes=64, offset=2048)
             w_tiles.append(w_packed)
             own = QUERIES - SHARE
             nc.vector.tensor_tensor(
@@ -206,7 +207,7 @@ def tile_attend_silu_gate_kernel(tc, qT, kT, vT, vs, kb, og, offs, out):
                 nc.gpsimd.tensor_scalar(
                     pairs[:, t // 2, :, t % 2], p_tiles[g][:, t, :], vs_cols[:, g, t : t + 1], 0.0, MULT, ADD
                 )
-            w_packed = keep.tile([P, QUERIES, PACK], BF16, name="w_first", tag="w_then_v", align_bytes=64)
+            w_packed = tail.tile([P, QUERIES, PACK], BF16, name="w_first", align_bytes=64, offset=0)
             w_tiles.append(w_packed)
             nc.scalar.copy(
                 w_packed[:].rearrange("p q t -> p (q t)").bitcast(F32).rearrange("p (q u) -> p q u", u=2),
@@ -215,8 +216,7 @@ def tile_attend_silu_gate_kernel(tc, qT, kT, vT, vs, kb, og, offs, out):
 
         def quantize_weights(g, q_cols):
             if len(w_codes) == g:
-                tag = "p1" if g == 0 else "w_codes"
-                w_codes.append(keep.tile([P, QUERIES], U32, name="w_codes%d" % g, tag=tag, align_bytes=64))
+                w_codes.append(keep.tile([P, QUERIES], U32, name="w_codes%d" % g, align_bytes=64))
             nc.vector.quantize_mx(
                 out=w_codes[g][:, q_cols].bitcast(FP8X4),
                 scales=w_scales[:, g, q_cols],
@@ -224,7 +224,7 @@ def tile_attend_silu_gate_kernel(tc, qT, kT, vT, vs, kb, og, offs, out):
             )
 
         def gather_values(g):
-            v_picked = w_second[:, 0:PASS] if g == 0 else v_second[:]
+            v_picked = v_first[:] if g == 0 else v_second[:]
             nc.vector.tensor_copy(
                 v_picked.rearrange("p (u m e) -> p m u e", u=2, e=2),
                 v_pool[:].indirect(offsets[:, 32 * g : 32 * g + 32]),
@@ -239,8 +239,10 @@ def tile_attend_silu_gate_kernel(tc, qT, kT, vT, vs, kb, og, offs, out):
             )
 
         def quantize_values(g):
-            tag = "v_codes" if g == 0 else "w_then_v"
-            v_codes.append(keep.tile([P, V_FEATURES], U32, name="v_codes%d" % g, tag=tag, align_bytes=64))
+            if g == 0:
+                v_codes.append(keep.tile([P, V_FEATURES], U32, name="v_codes0", align_bytes=64))
+            else:
+                v_codes.append(tail.tile([P, V_FEATURES], U32, name="v_codes1", align_bytes=64, offset=0))
             nc.vector.quantize_mx(
                 out=v_codes[g][:].bitcast(FP8X4),
                 scales=v_scales[:, g, :],

@@ -34,7 +34,7 @@ PIECES = 2
 PIECE_STEP = 64
 KB_PART = 0
 VS_PART = 4
-SHARE = 80
+SHARE = 48
 
 
 def tile_attend_silu_gate_kernel(tc, qT, kT, vT, vs, kb, og, offs, out):

@@ -34,7 +34,7 @@ PIECES = 2
 PIECE_STEP = 64
 KB_PART = 0
 VS_PART = 4
-SHARE = 48
+SHARE = 64
 
 
 def tile_attend_silu_gate_kernel(tc, qT, kT, vT, vs, kb, og, offs, out):
@@ -83,8 +83,6 @@ def tile_attend_silu_gate_kernel(tc, qT, kT, vT, vs, kb, og, offs, out):
 
         gate = keep.tile([P, Q_BLOCKS, V_FEATURES], F32, name="gate")
         nc.scalar.activation(gate[:], gate_in[:], SIGMOID)
-        warm = keep.tile([P, 1], F32, name="warm")
-        nc.scalar.activation(warm[:], gate[:, 0, 0:1], SILU)
 
         k_packed = [
             keep.tile([P, PACK, P, PACK], BF16, name="k_packed%d" % g, tag="k_stage%d" % g, align_bytes=64)

@@ -137,7 +137,7 @@ def tile_attend_silu_gate_kernel(tc, qT, kT, vT, vs, kb, og, offs, out):
         nc.tensor.transpose(vs_back[:], vs_turned[:], ident[:])
         gather_keys_half(2, 0)
         gather_keys_half(2, 1)
-        q_packed = keep.tile([P, QUERIES, PACK], BF16, name="q_packed", tag="q_then_k", align_bytes=64)
+        q_packed = tail.tile([P, QUERIES, PACK], BF16, name="q_packed", align_bytes=64, offset=4096)
         q_codes = keep.tile([P, QUERIES], U32, name="q_codes", align_bytes=64)
         q_scales = keep.tile([P, QUERIES], U8, name="q_scales", align_bytes=64)
         nc.scalar.copy(
@@ -147,8 +147,8 @@ def tile_attend_silu_gate_kernel(tc, qT, kT, vT, vs, kb, og, offs, out):
 
         k_codes = {}
 
-        def quantize_keys(g, t0, t1, tag):
-            codes = keep.tile([P, P * (t1 - t0)], U32, name="k_codes%d_%d" % (g, t0), tag=tag, align_bytes=64)
+        def quantize_keys(g, t0, t1, pool, **place):
+            codes = pool.tile([P, P * (t1 - t0)], U32, name="k_codes%d_%d" % (g, t0), align_bytes=64, **place)
             for t in range(t0, t1):
                 k_codes[g, t] = codes[:, P * (t - t0) : P * (t - t0 + 1)]
             nc.vector.quantize_mx(
@@ -249,13 +249,14 @@ def tile_attend_silu_gate_kernel(tc, qT, kT, vT, vs, kb, og, offs, out):
 
         gather_keys_half(3, 0)
         gather_keys_half(3, 1)
-        quantize_keys(0, 0, 2, "k_first")
+        quantize_keys(0, 0, 1, keep)
         nc.vector.quantize_mx(
             out=q_codes[:].bitcast(FP8X4), scales=q_scales[:], in_=q_packed[:].rearrange("p q j -> p (q j)")
         )
-        quantize_keys(0, 2, 4, "q_then_k")
+        quantize_keys(0, 1, 2, tail, offset=4096)
+        quantize_keys(0, 2, 4, tail, offset=4096 + 512)
         score(0)
-        quantize_keys(1, 0, 4, "k_stage0")
+        quantize_keys(1, 0, 4, keep, tag="k_stage0")
         score(1)
         gather_values(0)
         gather_values(1)

@@ -34,7 +34,6 @@ PIECES = 2
 PIECE_STEP = 64
 KB_PART = 0
 VS_PART = 4
-SHARE = 64
 
 
 def tile_attend_silu_gate_kernel(tc, qT, kT, vT, vs, kb, og, offs, out):
@@ -111,24 +110,28 @@ def tile_attend_silu_gate_kernel(tc, qT, kT, vT, vs, kb, og, offs, out):
             picked = keep.tile([P, SLOTS], F32, name=name + "_picked")
             nc.vector.tensor_copy(picked[:], row[:].indirect(offsets[:]))
             parts = keep.tile([P, PASSES, PACK, PIECES], F32, name=name + "_parts")
-            cols = keep.tile([P, PASSES, PACK], F32, name=name + "_cols")
             for g in range(PASSES):
                 turned = turn_psum.tile([P, PACK, P], F32, name="turned", tag="turned")
                 for t in range(PACK):
                     nc.tensor.transpose(turned[:, t, :], picked[:, PASS * g + t : PASS * (g + 1) : PACK], ident[:])
                 nc.scalar.copy(parts[:, g, :, :], turned[:, :, first:P:PIECE_STEP])
-            nc.gpsimd.tensor_tensor(cols[:], parts[:, :, :, 0], parts[:, :, :, 1], ADD)
-            return cols
+            return parts[:].rearrange("p g t h -> p (g t) h")
 
         gather_keys_plain(0)
-        kb_cols = columns(kb_row, KB_PART, "kb")
+        kb_parts = columns(kb_row, KB_PART, "kb")
+        kb_first = tail.tile([P, 144], F32, name="kb_first", offset=2560 - 32)
+        kb_rest = keep.tile([P, PASSES * PACK], F32, name="kb_rest")
+        nc.gpsimd.tensor_tensor(kb_first[:, 0:2], kb_parts[:, 0:2, 0], kb_parts[:, 0:2, 1], ADD)
+        nc.gpsimd.tensor_tensor(kb_rest[:, 2:], kb_parts[:, 2:, 0], kb_parts[:, 2:, 1], ADD)
         gather_keys_plain(1)
         for g in range(PASSES):
             interleave_keys(g)
-        vs_cols = columns(vs_row, VS_PART, "vs")
+        vs_parts = columns(vs_row, VS_PART, "vs")
+        vs_cols = keep.tile([P, PASSES * PACK], F32, name="vs_cols")
+        nc.gpsimd.tensor_tensor(vs_cols[:], vs_parts[:, :, 0], vs_parts[:, :, 1], ADD)
         vs_wide = keep.tile([P, P], F32, name="vs_wide")
-        nc.gpsimd.memset(vs_wide[:, PACK:P], 0.0)
-        nc.gpsimd.tensor_copy(vs_wide[:, 0:PACK], vs_cols[:, PASSES - 1, :])
+        nc.gpsimd.memset(vs_wide[:, PASSES * PACK : P], 0.0)
+        nc.gpsimd.tensor_copy(vs_wide[:, 0 : PASSES * PACK], vs_cols[:])
         vs_there = turn_psum.tile([P, P], F32, name="vs_there", tag="turned")
         nc.tensor.transpose(vs_there[:], vs_wide[:], ident[:])
         vs_turned = keep.tile([P, P], F32, name="vs_turned")
@@ -159,7 +162,7 @@ def tile_attend_silu_gate_kernel(tc, qT, kT, vT, vs, kb, og, offs, out):
 
         p_tiles = [keep.tile([P, PACK, QUERIES], F32, name="p_tile%d" % g, tag="p%d" % g, align_bytes=64) for g in range(PASSES)]
         v_first = tail.tile([P, PASS], BF16, name="v_first", align_bytes=64, offset=1536)
-        v_second = keep.tile([P, PASS], BF16, name="v_second", align_bytes=64)
+        v_second = tail.tile([P, PASS], BF16, name="v_second", align_bytes=64, offset=3072)
         v_tiles = [half.tile([P, V_FEATURES, PACK], BF16, name="v_packed%d" % g, align_bytes=64) for g in range(PASSES)]
         w_codes = []
         w_scales = keep.tile([P, PASSES, QUERIES], U8, name="w_scales", align_bytes=64)
@@ -178,47 +181,41 @@ def tile_attend_silu_gate_kernel(tc, qT, kT, vT, vs, kb, og, offs, out):
                     start=True,
                     stop=True,
                 )
-                nc.scalar.activation(p_tiles[g][:, t, :], bank[:], SILU, bias=kb_cols[:, g, t : t + 1])
+                col = PACK * g + t
+                biases = kb_first if col < 2 else kb_rest
+                nc.scalar.activation(p_tiles[g][:, t, :], bank[:], SILU, bias=biases[:, col : col + 1])
 
-        w_tiles = []
+        w_first = tail.tile([P, QUERIES, PACK], BF16, name="w_first", align_bytes=64, offset=0)
+        w_own = tail.tile([P, P, PACK], BF16, name="w_own", align_bytes=64, offset=2048)
+        w_shared = keep.tile([P, P, PACK], BF16, name="w_shared", align_bytes=64)
+        pairs_first = keep.tile([P, 2, QUERIES, 2], BF16, name="w_pairs")
 
-        def weigh(g):
-            w_packed = tail.tile([P, QUERIES, PACK], BF16, name="w_second", align_bytes=64, offset=2048)
-            w_tiles.append(w_packed)
-            own = QUERIES - SHARE
-            nc.vector.tensor_tensor(
-                w_packed[:, 0:own, :].rearrange("p (c i) t -> p c t i", i=RUN),
-                p_tiles[g][:, :, 0:own].rearrange("p t (c i) -> p c t i", i=RUN),
-                vs_back[:, 0:PACK].unsqueeze(1).unsqueeze(3).to_broadcast([P, own // RUN, PACK, RUN]),
+        def weigh(engine, target, g, q_cols, places, scales):
+            count = places.stop - places.start
+            width = q_cols.stop - q_cols.start
+            engine.tensor_tensor(
+                target.rearrange("p (c i) t -> p c t i", i=RUN),
+                p_tiles[g][:, places, q_cols].rearrange("p t (c i) -> p c t i", i=RUN),
+                scales[:, PACK * g + places.start : PACK * g + places.stop]
+                .unsqueeze(1)
+                .unsqueeze(3)
+                .to_broadcast([P, width // RUN, count, RUN]),
                 MULT,
             )
-            nc.gpsimd.tensor_tensor(
-                w_packed[:, own:QUERIES, :].rearrange("p (c i) t -> p c t i", i=RUN),
-                p_tiles[g][:, :, own:QUERIES].rearrange("p t (c i) -> p c t i", i=RUN),
-                vs_cols[:, g, :].unsqueeze(1).unsqueeze(3).to_broadcast([P, SHARE // RUN, PACK, RUN]),
-                MULT,
-            )
 
-        def weigh_in_pairs(g):
-            pairs = keep.tile([P, 2, QUERIES, 2], BF16, name="w_pairs")
-            for t in range(PACK):
-                nc.gpsimd.tensor_scalar(
-                    pairs[:, t // 2, :, t % 2], p_tiles[g][:, t, :], vs_cols[:, g, t : t + 1], 0.0, MULT, ADD
-                )
-            w_packed = tail.tile([P, QUERIES, PACK], BF16, name="w_first", align_bytes=64, offset=0)
-            w_tiles.append(w_packed)
+        def weave_first():
             nc.scalar.copy(
-                w_packed[:].rearrange("p q t -> p (q t)").bitcast(F32).rearrange("p (q u) -> p q u", u=2),
-                pairs[:].rearrange("p u q e -> p u (q e)").bitcast(F32).rearrange("p u q -> p q u"),
+                w_first[:].rearrange("p q t -> p (q t)").bitcast(F32).rearrange("p (q u) -> p q u", u=2),
+                pairs_first[:].rearrange("p u q e -> p u (q e)").bitcast(F32).rearrange("p u q -> p q u"),
             )
 
-        def quantize_weights(g, q_cols):
+        def quantize_weights(g, q_cols, source):
             if len(w_codes) == g:
                 w_codes.append(keep.tile([P, QUERIES], U32, name="w_codes%d" % g, align_bytes=64))
             nc.vector.quantize_mx(
                 out=w_codes[g][:, q_cols].bitcast(FP8X4),
                 scales=w_scales[:, g, q_cols],
-                in_=w_tiles[g][:, q_cols, :].rearrange("p q t -> p (q t)"),
+                in_=source.rearrange("p q t -> p (q t)"),
             )
 
         def gather_values(g):
@@ -258,15 +255,21 @@ def tile_attend_silu_gate_kernel(tc, qT, kT, vT, vs, kb, og, offs, out):
         score(0)
         quantize_keys(1, 0, 4, keep, tag="k_stage0")
         score(1)
+        weigh(nc.vector, pairs_first[:, 0, :, :], 0, slice(0, QUERIES), slice(0, 2), vs_back)
+        for t in range(2, PACK):
+            nc.gpsimd.tensor_scalar(
+                pairs_first[:, 1, :, t % 2], p_tiles[0][:, t, :], vs_cols[:, t : t + 1], 0.0, MULT, ADD
+            )
+        weigh(nc.gpsimd, w_shared[:], 1, slice(P, QUERIES), slice(0, PACK), vs_cols)
         gather_values(0)
         gather_values(1)
-        weigh_in_pairs(0)
-        weigh(1)
-        quantize_weights(0, slice(0, QUERIES))
+        weave_first()
+        weigh(nc.vector, w_own[:], 1, slice(0, P), slice(0, PACK), vs_back)
+        quantize_weights(0, slice(0, QUERIES), w_first[:])
         quantize_values(0)
-        quantize_weights(1, slice(0, P))
+        quantize_weights(1, slice(0, P), w_own[:])
+        quantize_weights(1, slice(P, QUERIES), w_shared[:])
         quantize_values(1)
-        quantize_weights(1, slice(P, QUERIES))
 
         for b in range(Q_BLOCKS):
             q_cols = slice(P * b, P * (b + 1))

@@ -34,6 +34,7 @@ PIECES = 2
 PIECE_STEP = 64
 KB_PART = 0
 VS_PART = 4
+SHARE = 96
 
 
 def tile_attend_silu_gate_kernel(tc, qT, kT, vT, vs, kb, og, offs, out):
@@ -52,7 +53,7 @@ def tile_attend_silu_gate_kernel(tc, qT, kT, vT, vs, kb, og, offs, out):
         vs_row = keep.tile([P, TOKENS], F32, name="vs_row")
         k_planes = [keep.tile([P, TOKENS], F32, name="k_plane%d" % j) for j in range(PACK)]
         v_pool = keep.tile([P, TOKENS], F32, name="v_pool")
-        q_raw = keep.tile([P, PACK, QUERIES], F32, name="q_raw")
+        q_raw = tail.tile([P, PACK, QUERIES], F32, name="q_raw", align_bytes=64, offset=8192)
         gate_in = keep.tile([P, Q_BLOCKS, V_FEATURES], F32, name="gate_in")
 
         k_rows = kT.rearrange("(p j) n -> j p n", j=PACK)
@@ -82,10 +83,13 @@ def tile_attend_silu_gate_kernel(tc, qT, kT, vT, vs, kb, og, offs, out):
 
         gate = keep.tile([P, Q_BLOCKS, V_FEATURES], F32, name="gate")
         nc.scalar.activation(gate[:], gate_in[:], SIGMOID)
+        warm = keep.tile([P, 1], F32, name="warm")
+        nc.scalar.activation(warm[:], gate[:, 0, 0:1], SILU)
 
+        k_pairs = [keep.tile([P, 2, PACK, P, 2], BF16, name="k_pairs%d" % g) for g in range(PASSES)]
         k_packed = [
-            keep.tile([P, PACK, P, PACK], BF16, name="k_packed%d" % g, tag="k_stage%d" % g, align_bytes=64)
-            for g in range(PASSES)
+            keep.tile([P, PACK, P, PACK], BF16, name="k_packed0", align_bytes=64),
+            tail.tile([P, PACK, P, PACK], BF16, name="k_packed1", align_bytes=64, offset=8192 + 2048),
         ]
         k_scales = keep.tile([P, SLOTS], U8, name="k_scales", align_bytes=64)
 
@@ -96,14 +100,20 @@ def tile_attend_silu_gate_kernel(tc, qT, kT, vT, vs, kb, og, offs, out):
 
         def interleave_keys(g):
             nc.scalar.copy(
-                k_packed[g][:, :, :, 0:2],
+                k_pairs[g][:, 0, :, :, :],
                 k_picked[:, :, PASS * g : PASS * (g + 1)].rearrange("p j (m t) -> p t m j", t=PACK),
             )
 
         def gather_keys_half(j, g):
             nc.vector.tensor_copy(
-                k_packed[g][:, :, :, j].rearrange("p t m -> p m t"),
+                k_pairs[g][:, 1, :, :, j % 2].rearrange("p t m -> p m t"),
                 k_planes[j][:].indirect(offsets[:, 32 * g : 32 * g + 32]),
+            )
+
+        def weave_keys(copy, g):
+            copy(
+                k_packed[g][:].rearrange("p t m j -> p (t m j)").bitcast(F32).rearrange("p (s u) -> p s u", u=2),
+                k_pairs[g][:].rearrange("p u t m e -> p u (t m e)").bitcast(F32).rearrange("p u s -> p s u"),
             )
 
         def columns(row, first, name):
@@ -119,10 +129,12 @@ def tile_attend_silu_gate_kernel(tc, qT, kT, vT, vs, kb, og, offs, out):
 
         gather_keys_plain(0)
         kb_parts = columns(kb_row, KB_PART, "kb")
-        kb_first = tail.tile([P, 144], F32, name="kb_first", offset=2560 - 32)
-        kb_rest = keep.tile([P, PASSES * PACK], F32, name="kb_rest")
+        kb_first = tail.tile([P, 16], F32, name="kb_first", offset=4096 - 32)
+        kb_mid = tail.tile([P, PASSES * PACK], F32, name="kb_mid", offset=0)
+        kb_last = keep.tile([P, PASSES * PACK], F32, name="kb_last")
         nc.gpsimd.tensor_tensor(kb_first[:, 0:2], kb_parts[:, 0:2, 0], kb_parts[:, 0:2, 1], ADD)
-        nc.gpsimd.tensor_tensor(kb_rest[:, 2:], kb_parts[:, 2:, 0], kb_parts[:, 2:, 1], ADD)
+        nc.gpsimd.tensor_tensor(kb_mid[:, 2:7], kb_parts[:, 2:7, 0], kb_parts[:, 2:7, 1], ADD)
+        nc.gpsimd.tensor_tensor(kb_last[:, 7:8], kb_parts[:, 7:8, 0], kb_parts[:, 7:8, 1], ADD)
         gather_keys_plain(1)
         for g in range(PASSES):
             interleave_keys(g)
@@ -140,7 +152,7 @@ def tile_attend_silu_gate_kernel(tc, qT, kT, vT, vs, kb, og, offs, out):
         nc.tensor.transpose(vs_back[:], vs_turned[:], ident[:])
         gather_keys_half(2, 0)
         gather_keys_half(2, 1)
-        q_packed = tail.tile([P, QUERIES, PACK], BF16, name="q_packed", align_bytes=64, offset=4096)
+        q_packed = tail.tile([P, QUERIES, PACK], BF16, name="q_packed", align_bytes=64, offset=5120)
         q_codes = keep.tile([P, QUERIES], U32, name="q_codes", align_bytes=64)
         q_scales = keep.tile([P, QUERIES], U8, name="q_scales", align_bytes=64)
         nc.scalar.copy(
@@ -161,8 +173,9 @@ def tile_attend_silu_gate_kernel(tc, qT, kT, vT, vs, kb, og, offs, out):
             )
 
         p_tiles = [keep.tile([P, PACK, QUERIES], F32, name="p_tile%d" % g, tag="p%d" % g, align_bytes=64) for g in range(PASSES)]
-        v_first = tail.tile([P, PASS], BF16, name="v_first", align_bytes=64, offset=1536)
-        v_second = tail.tile([P, PASS], BF16, name="v_second", align_bytes=64, offset=3072)
+        w_second = tail.tile([P, QUERIES, PACK], BF16, name="w_second", align_bytes=64, offset=2048)
+        v_first = w_second[:, 0:P, :].rearrange("p q t -> p (q t)")
+        v_second = tail.tile([P, PASS], BF16, name="v_second", align_bytes=64, offset=4096)
         v_tiles = [half.tile([P, V_FEATURES, PACK], BF16, name="v_packed%d" % g, align_bytes=64) for g in range(PASSES)]
         w_codes = []
         w_scales = keep.tile([P, PASSES, QUERIES], U8, name="w_scales", align_bytes=64)
@@ -182,12 +195,11 @@ def tile_attend_silu_gate_kernel(tc, qT, kT, vT, vs, kb, og, offs, out):
                     stop=True,
                 )
                 col = PACK * g + t
-                biases = kb_first if col < 2 else kb_rest
+                biases = kb_first if col < 2 else kb_mid if col < 7 else kb_last
                 nc.scalar.activation(p_tiles[g][:, t, :], bank[:], SILU, bias=biases[:, col : col + 1])
 
         w_first = tail.tile([P, QUERIES, PACK], BF16, name="w_first", align_bytes=64, offset=0)
-        w_own = tail.tile([P, P, PACK], BF16, name="w_own", align_bytes=64, offset=2048)
-        w_shared = keep.tile([P, P, PACK], BF16, name="w_shared", align_bytes=64)
+        own = QUERIES - SHARE
         pairs_first = keep.tile([P, 2, QUERIES, 2], BF16, name="w_pairs")
 
         def weigh(engine, target, g, q_cols, places, scales):
@@ -211,7 +223,9 @@ def tile_attend_silu_gate_kernel(tc, qT, kT, vT, vs, kb, og, offs, out):
 
         def quantize_weights(g, q_cols, source):
             if len(w_codes) == g:
-                w_codes.append(keep.tile([P, QUERIES], U32, name="w_codes%d" % g, align_bytes=64))
+                w_codes.append(
+                    keep.tile([P, QUERIES], U32, name="w_codes%d" % g, tag="p1" if g == 1 else "w0", align_bytes=64)
+                )
             nc.vector.quantize_mx(
                 out=w_codes[g][:, q_cols].bitcast(FP8X4),
                 scales=w_scales[:, g, q_cols],
@@ -219,7 +233,7 @@ def tile_attend_silu_gate_kernel(tc, qT, kT, vT, vs, kb, og, offs, out):
             )
 
         def gather_values(g):
-            v_picked = v_first[:] if g == 0 else v_second[:]
+            v_picked = v_first if g == 0 else v_second[:]
             nc.vector.tensor_copy(
                 v_picked.rearrange("p (u m e) -> p m u e", u=2, e=2),
                 v_pool[:].indirect(offsets[:, 32 * g : 32 * g + 32]),
@@ -246,30 +260,32 @@ def tile_attend_silu_gate_kernel(tc, qT, kT, vT, vs, kb, og, offs, out):
 
         gather_keys_half(3, 0)
         gather_keys_half(3, 1)
-        quantize_keys(0, 0, 1, keep)
+        weave_keys(nc.vector.tensor_copy, 0)
+        weave_keys(nc.scalar.copy, 1)
         nc.vector.quantize_mx(
             out=q_codes[:].bitcast(FP8X4), scales=q_scales[:], in_=q_packed[:].rearrange("p q j -> p (q j)")
         )
-        quantize_keys(0, 1, 2, tail, offset=4096)
-        quantize_keys(0, 2, 4, tail, offset=4096 + 512)
+        quantize_keys(0, 0, 1, tail, offset=8192)
+        quantize_keys(0, 1, 2, tail, offset=8192 + 512)
+        quantize_keys(0, 2, 4, tail, offset=8192 + 1024)
         score(0)
-        quantize_keys(1, 0, 4, keep, tag="k_stage0")
+        quantize_keys(1, 0, 4, keep)
         score(1)
         weigh(nc.vector, pairs_first[:, 0, :, :], 0, slice(0, QUERIES), slice(0, 2), vs_back)
         for t in range(2, PACK):
             nc.gpsimd.tensor_scalar(
                 pairs_first[:, 1, :, t % 2], p_tiles[0][:, t, :], vs_cols[:, t : t + 1], 0.0, MULT, ADD
             )
-        weigh(nc.gpsimd, w_shared[:], 1, slice(P, QUERIES), slice(0, PACK), vs_cols)
+        weigh(nc.gpsimd, w_second[:, own:QUERIES, :], 1, slice(own, QUERIES), slice(0, PACK), vs_cols)
+        weave_first()
         gather_values(0)
         gather_values(1)
-        weave_first()
-        weigh(nc.vector, w_own[:], 1, slice(0, P), slice(0, PACK), vs_back)
+        weigh(nc.vector, w_second[:, 0:own, :], 1, slice(0, own), slice(0, PACK), vs_back)
         quantize_weights(0, slice(0, QUERIES), w_first[:])
         quantize_values(0)
-        quantize_weights(1, slice(0, P), w_own[:])
-        quantize_weights(1, slice(P, QUERIES), w_shared[:])
+        quantize_weights(1, slice(0, P), w_second[:, 0:P, :])
         quantize_values(1)
+        quantize_weights(1, slice(P, QUERIES), w_second[:, P:QUERIES, :])
 
         for b in range(Q_BLOCKS):
             q_cols = slice(P * b, P * (b + 1))

@@ -34,7 +34,7 @@ PIECES = 2
 PIECE_STEP = 64
 KB_PART = 0
 VS_PART = 4
-SHARE = 96
+SHARE = 32
 
 
 def tile_attend_silu_gate_kernel(tc, qT, kT, vT, vs, kb, og, offs, out):
@@ -53,7 +53,7 @@ def tile_attend_silu_gate_kernel(tc, qT, kT, vT, vs, kb, og, offs, out):
         vs_row = keep.tile([P, TOKENS], F32, name="vs_row")
         k_planes = [keep.tile([P, TOKENS], F32, name="k_plane%d" % j) for j in range(PACK)]
         v_pool = keep.tile([P, TOKENS], F32, name="v_pool")
-        q_raw = tail.tile([P, PACK, QUERIES], F32, name="q_raw", align_bytes=64, offset=8192)
+        q_raw = tail.tile([P, PACK, QUERIES], F32, name="q_raw", align_bytes=64, offset=10240)
         gate_in = keep.tile([P, Q_BLOCKS, V_FEATURES], F32, name="gate_in")
 
         k_rows = kT.rearrange("(p j) n -> j p n", j=PACK)
@@ -87,10 +87,12 @@ def tile_attend_silu_gate_kernel(tc, qT, kT, vT, vs, kb, og, offs, out):
         nc.scalar.activation(warm[:], gate[:, 0, 0:1], SILU)
 
         k_pairs = [keep.tile([P, 2, PACK, P, 2], BF16, name="k_pairs%d" % g) for g in range(PASSES)]
-        k_packed = [
-            keep.tile([P, PACK, P, PACK], BF16, name="k_packed0", align_bytes=64),
-            tail.tile([P, PACK, P, PACK], BF16, name="k_packed1", align_bytes=64, offset=8192 + 2048),
-        ]
+        k_packed = {
+            (0, 0): keep.tile([P, 2, P, PACK], BF16, name="k_packed00", align_bytes=64),
+            (0, 1): tail.tile([P, 2, P, PACK], BF16, name="k_packed01", align_bytes=64, offset=11328),
+            (1, 0): tail.tile([P, 2, P, PACK], BF16, name="k_packed10", align_bytes=64, offset=13376),
+            (1, 1): tail.tile([P, 2, P, PACK], BF16, name="k_packed11", align_bytes=64, offset=8256),
+        }
         k_scales = keep.tile([P, SLOTS], U8, name="k_scales", align_bytes=64)
 
         k_picked = keep.tile([P, 2, SLOTS], F32, name="k_picked")
@@ -110,10 +112,13 @@ def tile_attend_silu_gate_kernel(tc, qT, kT, vT, vs, kb, og, offs, out):
                 k_planes[j][:].indirect(offsets[:, 32 * g : 32 * g + 32]),
             )
 
-        def weave_keys(copy, g):
+        def weave_keys(copy, g, h):
             copy(
-                k_packed[g][:].rearrange("p t m j -> p (t m j)").bitcast(F32).rearrange("p (s u) -> p s u", u=2),
-                k_pairs[g][:].rearrange("p u t m e -> p u (t m e)").bitcast(F32).rearrange("p u s -> p s u"),
+                k_packed[g, h][:].rearrange("p t m j -> p (t m j)").bitcast(F32).rearrange("p (s u) -> p s u", u=2),
+                k_pairs[g][:, :, 2 * h : 2 * h + 2, :, :]
+                .rearrange("p u t m e -> p u (t m e)")
+                .bitcast(F32)
+                .rearrange("p u s -> p s u"),
             )
 
         def columns(row, first, name):
@@ -129,8 +134,8 @@ def tile_attend_silu_gate_kernel(tc, qT, kT, vT, vs, kb, og, offs, out):
 
         gather_keys_plain(0)
         kb_parts = columns(kb_row, KB_PART, "kb")
-        kb_first = tail.tile([P, 16], F32, name="kb_first", offset=4096 - 32)
-        kb_mid = tail.tile([P, PASSES * PACK], F32, name="kb_mid", offset=0)
+        kb_first = tail.tile([P, 160], F32, name="kb_first", offset=4096 + 992)
+        kb_mid = tail.tile([P, 16], F32, name="kb_mid", offset=1024 - 32)
         kb_last = keep.tile([P, PASSES * PACK], F32, name="kb_last")
         nc.gpsimd.tensor_tensor(kb_first[:, 0:2], kb_parts[:, 0:2, 0], kb_parts[:, 0:2, 1], ADD)
         nc.gpsimd.tensor_tensor(kb_mid[:, 2:7], kb_parts[:, 2:7, 0], kb_parts[:, 2:7, 1], ADD)
@@ -152,7 +157,7 @@ def tile_attend_silu_gate_kernel(tc, qT, kT, vT, vs, kb, og, offs, out):
         nc.tensor.transpose(vs_back[:], vs_turned[:], ident[:])
         gather_keys_half(2, 0)
         gather_keys_half(2, 1)
-        q_packed = tail.tile([P, QUERIES, PACK], BF16, name="q_packed", align_bytes=64, offset=5120)
+        q_packed = tail.tile([P, QUERIES, PACK], BF16, name="q_packed", align_bytes=64, offset=15424)
         q_codes = keep.tile([P, QUERIES], U32, name="q_codes", align_bytes=64)
         q_scales = keep.tile([P, QUERIES], U8, name="q_scales", align_bytes=64)
         nc.scalar.copy(
@@ -169,21 +174,20 @@ def tile_attend_silu_gate_kernel(tc, qT, kT, vT, vs, kb, og, offs, out):
             nc.vector.quantize_mx(
                 out=codes[:].bitcast(FP8X4),
                 scales=k_scales[:, PASS * g + P * t0 : PASS * g + P * t1],
-                in_=k_packed[g][:, t0:t1, :, :].rearrange("p t m j -> p (t m j)"),
+                in_=k_packed[g, t0 // 2][:, t0 % 2 : t0 % 2 + t1 - t0, :, :].rearrange("p t m j -> p (t m j)"),
             )
 
         p_tiles = [keep.tile([P, PACK, QUERIES], F32, name="p_tile%d" % g, tag="p%d" % g, align_bytes=64) for g in range(PASSES)]
-        w_second = tail.tile([P, QUERIES, PACK], BF16, name="w_second", align_bytes=64, offset=2048)
-        v_first = w_second[:, 0:P, :].rearrange("p q t -> p (q t)")
-        v_second = tail.tile([P, PASS], BF16, name="v_second", align_bytes=64, offset=4096)
+        v_first = tail.tile([P, PASS], BF16, name="v_first", align_bytes=64, offset=4096)
+        v_second = tail.tile([P, PASS], BF16, name="v_second", align_bytes=64, offset=4096 + 1600)
         v_tiles = [half.tile([P, V_FEATURES, PACK], BF16, name="v_packed%d" % g, align_bytes=64) for g in range(PASSES)]
         w_codes = []
         w_scales = keep.tile([P, PASSES, QUERIES], U8, name="w_scales", align_bytes=64)
         v_codes = []
         v_scales = keep.tile([P, PASSES, V_FEATURES], U8, name="v_scales", align_bytes=64)
 
-        def score(g):
-            for t in range(PACK):
+        def score(g, h):
+            for t in range(2 * h, 2 * h + 2):
                 bank = score_psum.tile([P, QUERIES], F32, name="bank")
                 nc.tensor.matmul_mx(
                     out=bank[:],
@@ -198,8 +202,9 @@ def tile_attend_silu_gate_kernel(tc, qT, kT, vT, vs, kb, og, offs, out):
                 biases = kb_first if col < 2 else kb_mid if col < 7 else kb_last
                 nc.scalar.activation(p_tiles[g][:, t, :], bank[:], SILU, bias=biases[:, col : col + 1])
 
-        w_first = tail.tile([P, QUERIES, PACK], BF16, name="w_first", align_bytes=64, offset=0)
-        own = QUERIES - SHARE
+        w_first = tail.tile([P, QUERIES, PACK], BF16, name="w_first", align_bytes=64, offset=1024)
+        w_own = tail.tile([P, P, PACK], BF16, name="w_own", align_bytes=64, offset=4096 - 960)
+        w_shared = tail.tile([P, P, PACK], BF16, name="w_shared", align_bytes=64, offset=0)
         pairs_first = keep.tile([P, 2, QUERIES, 2], BF16, name="w_pairs")
 
         def weigh(engine, target, g, q_cols, places, scales):
@@ -223,9 +228,10 @@ def tile_attend_silu_gate_kernel(tc, qT, kT, vT, vs, kb, og, offs, out):
 
         def quantize_weights(g, q_cols, source):
             if len(w_codes) == g:
-                w_codes.append(
-                    keep.tile([P, QUERIES], U32, name="w_codes%d" % g, tag="p1" if g == 1 else "w0", align_bytes=64)
-                )
+                if g == 0:
+                    w_codes.append(tail.tile([P, QUERIES], U32, name="w_codes0", align_bytes=64, offset=4096 + 576))
+                else:
+                    w_codes.append(keep.tile([P, QUERIES], U32, name="w_codes1", tag="p1", align_bytes=64))
             nc.vector.quantize_mx(
                 out=w_codes[g][:, q_cols].bitcast(FP8X4),
                 scales=w_scales[:, g, q_cols],
@@ -233,7 +239,7 @@ def tile_attend_silu_gate_kernel(tc, qT, kT, vT, vs, kb, og, offs, out):
             )
 
         def gather_values(g):
-            v_picked = v_first if g == 0 else v_second[:]
+            v_picked = v_first[:] if g == 0 else v_second[:]
             nc.vector.tensor_copy(
                 v_picked.rearrange("p (u m e) -> p m u e", u=2, e=2),
                 v_pool[:].indirect(offsets[:, 32 * g : 32 * g + 32]),
@@ -249,9 +255,9 @@ def tile_attend_silu_gate_kernel(tc, qT, kT, vT, vs, kb, og, offs, out):
 
         def quantize_values(g):
             if g == 0:
-                v_codes.append(keep.tile([P, V_FEATURES], U32, name="v_codes0", align_bytes=64))
+                v_codes.append(tail.tile([P, V_FEATURES], U32, name="v_codes0", align_bytes=64, offset=4096 + 64))
             else:
-                v_codes.append(tail.tile([P, V_FEATURES], U32, name="v_codes1", align_bytes=64, offset=0))
+                v_codes.append(tail.tile([P, V_FEATURES], U32, name="v_codes1", align_bytes=64, offset=1024))
             nc.vector.quantize_mx(
                 out=v_codes[g][:].bitcast(FP8X4),
                 scales=v_scales[:, g, :],
@@ -260,32 +266,40 @@ def tile_attend_silu_gate_kernel(tc, qT, kT, vT, vs, kb, og, offs, out):
 
         gather_keys_half(3, 0)
         gather_keys_half(3, 1)
-        weave_keys(nc.vector.tensor_copy, 0)
-        weave_keys(nc.scalar.copy, 1)
+        weave_keys(nc.vector.tensor_copy, 0, 0)
+        weave_keys(nc.scalar.copy, 1, 0)
+        weave_keys(nc.scalar.copy, 1, 1)
         nc.vector.quantize_mx(
             out=q_codes[:].bitcast(FP8X4), scales=q_scales[:], in_=q_packed[:].rearrange("p q j -> p (q j)")
         )
-        quantize_keys(0, 0, 1, tail, offset=8192)
-        quantize_keys(0, 1, 2, tail, offset=8192 + 512)
-        quantize_keys(0, 2, 4, tail, offset=8192 + 1024)
-        score(0)
-        quantize_keys(1, 0, 4, keep)
-        score(1)
+        quantize_keys(0, 0, 1, tail, offset=10304)
+        quantize_keys(0, 1, 2, tail, offset=10816)
+        weave_keys(nc.vector.tensor_copy, 0, 1)
+        quantize_keys(1, 0, 2, keep)
+        quantize_keys(0, 2, 4, keep)
+        quantize_keys(1, 2, 4, keep)
+        for h in range(2):
+            for g in range(PASSES):
+                score(g, h)
         weigh(nc.vector, pairs_first[:, 0, :, :], 0, slice(0, QUERIES), slice(0, 2), vs_back)
         for t in range(2, PACK):
             nc.gpsimd.tensor_scalar(
                 pairs_first[:, 1, :, t % 2], p_tiles[0][:, t, :], vs_cols[:, t : t + 1], 0.0, MULT, ADD
             )
-        weigh(nc.gpsimd, w_second[:, own:QUERIES, :], 1, slice(own, QUERIES), slice(0, PACK), vs_cols)
+        weigh(nc.gpsimd, w_shared[:, SHARE:P, :], 1, slice(P + SHARE, QUERIES), slice(0, PACK), vs_cols)
         weave_first()
+        for t in range(PACK):
+            nc.scalar.activation(
+                w_shared[:, 0:SHARE, t], p_tiles[1][:, t, P : P + SHARE], COPY, scale=vs_cols[:, PACK + t : PACK + t + 1]
+            )
         gather_values(0)
         gather_values(1)
-        weigh(nc.vector, w_second[:, 0:own, :], 1, slice(0, own), slice(0, PACK), vs_back)
+        weigh(nc.vector, w_own[:], 1, slice(0, P), slice(0, PACK), vs_back)
         quantize_weights(0, slice(0, QUERIES), w_first[:])
         quantize_values(0)
-        quantize_weights(1, slice(0, P), w_second[:, 0:P, :])
+        quantize_weights(1, slice(0, P), w_own[:])
         quantize_values(1)
-        quantize_weights(1, slice(P, QUERIES), w_second[:, P:QUERIES, :])
+        quantize_weights(1, slice(P, QUERIES), w_shared[:])
 
         for b in range(Q_BLOCKS):
             q_cols = slice(P * b, P * (b + 1))

@@ -186,8 +186,8 @@ def tile_attend_silu_gate_kernel(tc, qT, kT, vT, vs, kb, og, offs, out):
         v_codes = []
         v_scales = keep.tile([P, PASSES, V_FEATURES], U8, name="v_scales", align_bytes=64)
 
-        def score(g, h):
-            for t in range(2 * h, 2 * h + 2):
+        def score(g, places):
+            for t in places:
                 bank = score_psum.tile([P, QUERIES], F32, name="bank")
                 nc.tensor.matmul_mx(
                     out=bank[:],
@@ -278,20 +278,21 @@ def tile_attend_silu_gate_kernel(tc, qT, kT, vT, vs, kb, og, offs, out):
         quantize_keys(1, 0, 2, keep)
         quantize_keys(0, 2, 4, keep)
         quantize_keys(1, 2, 4, keep)
-        for h in range(2):
-            for g in range(PASSES):
-                score(g, h)
+        score(0, range(0, 2))
+        score(1, range(0, 1))
+        score(0, range(2, PACK))
+        score(1, range(1, PACK))
         weigh(nc.vector, pairs_first[:, 0, :, :], 0, slice(0, QUERIES), slice(0, 2), vs_back)
         for t in range(2, PACK):
             nc.gpsimd.tensor_scalar(
                 pairs_first[:, 1, :, t % 2], p_tiles[0][:, t, :], vs_cols[:, t : t + 1], 0.0, MULT, ADD
             )
         weigh(nc.gpsimd, w_shared[:, SHARE:P, :], 1, slice(P + SHARE, QUERIES), slice(0, PACK), vs_cols)
-        weave_first()
         for t in range(PACK):
             nc.scalar.activation(
                 w_shared[:, 0:SHARE, t], p_tiles[1][:, t, P : P + SHARE], COPY, scale=vs_cols[:, PACK + t : PACK + t + 1]
             )
+        weave_first()
         gather_values(0)
         gather_values(1)
         weigh(nc.vector, w_own[:], 1, slice(0, P), slice(0, PACK), vs_back)

@@ -14,6 +14,7 @@ FLOPS = 2 * QUERIES * SLOTS * (FEATURES + V_FEATURES)
 F32 = mybir.dt.float32
 BF16 = mybir.dt.bfloat16
 U32 = mybir.dt.uint32
+I32 = mybir.dt.int32
 U16 = mybir.dt.uint16
 U8 = mybir.dt.uint8
 FP8X4 = mybir.dt.float8_e4m3fn_x4
@@ -58,10 +59,8 @@ def tile_attend_silu_gate_kernel(tc, qT, kT, vT, vs, kb, og, offs, out):
 
         k_rows = kT.rearrange("(p j) n -> j p n", j=PACK)
 
-        share = 3 * TOKENS // 4
         for row in (kb_row, vs_row):
-            nc.vector.memset(row[:, 0:share], 0.0)
-            nc.gpsimd.memset(row[:, share:TOKENS], 0.0)
+            nc.vector.memset(row[:].bitcast(I32), 0)
         make_identity(nc, ident[:])
         nc.scalar.dma_start(gate_in[:], og[0].rearrange("(p b) e -> p b e", b=Q_BLOCKS))
 

@@ -24,6 +24,7 @@ SIGMOID = mybir.ActivationFunctionType.Sigmoid
 SILU = mybir.ActivationFunctionType.Silu
 MULT = mybir.AluOpType.mult
 ADD = mybir.AluOpType.add
+X = mybir.AxisListType.X
 
 P = 128
 PACK = 4
@@ -35,18 +36,20 @@ PIECES = 2
 PIECE_STEP = 64
 KB_PART = 0
 VS_PART = 4
-SHARE = 32
+SHARE = 64
+EARLY_ROWS = 80
+Q_SPLIT = 40
 
 
 def tile_attend_silu_gate_kernel(tc, qT, kT, vT, vs, kb, og, offs, out):
     nc = tc.nc
     with ExitStack() as ctx:
         keep = ctx.enter_context(tc.tile_pool(name="keep", bufs=1))
-        half = ctx.enter_context(tc.tile_pool(name="half", bufs=2))
         tail = ctx.enter_context(tc.tile_pool(name="tail", bufs=1))
-        turn_psum = ctx.enter_context(tc.psum_pool(name="turn_psum", bufs=2))
-        score_psum = ctx.enter_context(tc.psum_pool(name="score_psum", bufs=4))
-        y_psum = ctx.enter_context(tc.psum_pool(name="y_psum", bufs=2))
+        psum = ctx.enter_context(tc.psum_pool(name="psum", bufs=1))
+
+        def bank(index, shape, name):
+            return psum.tile(shape, F32, name=name, tag="bank%d" % index)
 
         offsets = keep.tile([P, SLOTS // 16], U16, name="offsets")
         ident = keep.tile([P, P], F32, name="ident")
@@ -54,8 +57,8 @@ def tile_attend_silu_gate_kernel(tc, qT, kT, vT, vs, kb, og, offs, out):
         vs_row = keep.tile([P, TOKENS], F32, name="vs_row")
         k_planes = [keep.tile([P, TOKENS], F32, name="k_plane%d" % j) for j in range(PACK)]
         v_pool = keep.tile([P, TOKENS], F32, name="v_pool")
-        q_raw = tail.tile([P, PACK, QUERIES], F32, name="q_raw", align_bytes=64, offset=10240)
-        gate_in = keep.tile([P, Q_BLOCKS, V_FEATURES], F32, name="gate_in")
+        q_raw = keep.tile([P, PACK, QUERIES], F32, name="q_raw")
+        gate_in = tail.tile([P, Q_BLOCKS, V_FEATURES], F32, name="gate_in", align_bytes=64, offset=8192)
 
         k_rows = kT.rearrange("(p j) n -> j p n", j=PACK)
 
@@ -82,228 +85,187 @@ def tile_attend_silu_gate_kernel(tc, qT, kT, vT, vs, kb, og, offs, out):
 
         gate = keep.tile([P, Q_BLOCKS, V_FEATURES], F32, name="gate")
         nc.scalar.activation(gate[:], gate_in[:], SIGMOID)
-        warm = keep.tile([P, 1], F32, name="warm")
-        nc.scalar.activation(warm[:], gate[:, 0, 0:1], SILU)
+        warm_in = keep.tile([P, 1], F32, name="warm_in")
+        nc.gpsimd.memset(warm_in[:], 0.0)
+        warm = tail.tile([P, 1], F32, name="warm", align_bytes=64, offset=8192)
+        nc.scalar.activation(warm[:], warm_in[:], SILU)
 
-        k_pairs = [keep.tile([P, 2, PACK, P, 2], BF16, name="k_pairs%d" % g) for g in range(PASSES)]
-        k_packed = {
-            (0, 0): keep.tile([P, 2, P, PACK], BF16, name="k_packed00", align_bytes=64),
-            (0, 1): tail.tile([P, 2, P, PACK], BF16, name="k_packed01", align_bytes=64, offset=11328),
-            (1, 0): tail.tile([P, 2, P, PACK], BF16, name="k_packed10", align_bytes=64, offset=13376),
-            (1, 1): tail.tile([P, 2, P, PACK], BF16, name="k_packed11", align_bytes=64, offset=8256),
-        }
-        k_scales = keep.tile([P, SLOTS], U8, name="k_scales", align_bytes=64)
+        def gather(g, target, window):
+            picked = window[:].indirect(offsets[:, 32 * g : 32 * g + 32])
+            if g == 0:
+                nc.vector.tensor_copy(target, picked)
+            else:
+                nc.scalar.activation(target, picked, COPY)
 
-        k_picked = keep.tile([P, 2, SLOTS], F32, name="k_picked")
+        k_first = keep.tile([P, 2, 2, P, PACK], BF16, name="k_first", align_bytes=64)
+        k_second = keep.tile([P, 2, 4, P, PACK], BF16, name="k_second", align_bytes=64)
+        k_packed = [k_first[:], k_second[:, :, 0:2, :, :]]
 
-        def gather_keys_plain(j):
-            nc.vector.tensor_copy(k_picked[:, j, :], k_planes[j][:].indirect(offsets[:]))
-
-        def interleave_keys(g):
-            nc.scalar.copy(
-                k_pairs[g][:, 0, :, :, :],
-                k_picked[:, :, PASS * g : PASS * (g + 1)].rearrange("p j (m t) -> p t m j", t=PACK),
-            )
-
-        def gather_keys_half(j, g):
-            nc.vector.tensor_copy(
-                k_pairs[g][:, 1, :, :, j % 2].rearrange("p t m -> p m t"),
-                k_planes[j][:].indirect(offsets[:, 32 * g : 32 * g + 32]),
-            )
-
-        def weave_keys(copy, g, h):
-            copy(
-                k_packed[g, h][:].rearrange("p t m j -> p (t m j)").bitcast(F32).rearrange("p (s u) -> p s u", u=2),
-                k_pairs[g][:, :, 2 * h : 2 * h + 2, :, :]
-                .rearrange("p u t m e -> p u (t m e)")
-                .bitcast(F32)
-                .rearrange("p u s -> p s u"),
-            )
-
-        def columns(row, first, name):
-            picked = keep.tile([P, SLOTS], F32, name=name + "_picked")
-            nc.vector.tensor_copy(picked[:], row[:].indirect(offsets[:]))
-            parts = keep.tile([P, PASSES, PACK, PIECES], F32, name=name + "_parts")
+        def gather_keys(j):
             for g in range(PASSES):
-                turned = turn_psum.tile([P, PACK, P], F32, name="turned", tag="turned")
-                for t in range(PACK):
-                    nc.tensor.transpose(turned[:, t, :], picked[:, PASS * g + t : PASS * (g + 1) : PACK], ident[:])
-                nc.scalar.copy(parts[:, g, :, :], turned[:, :, first:P:PIECE_STEP])
-            return parts[:].rearrange("p g t h -> p (g t) h")
+                gather(g, k_packed[g][:, :, :, :, j].rearrange("p u e m -> p m u e"), k_planes[j])
 
-        gather_keys_plain(0)
-        kb_parts = columns(kb_row, KB_PART, "kb")
-        kb_first = tail.tile([P, 160], F32, name="kb_first", offset=4096 + 992)
-        kb_mid = tail.tile([P, 16], F32, name="kb_mid", offset=1024 - 32)
-        kb_last = keep.tile([P, PASSES * PACK], F32, name="kb_last")
-        nc.gpsimd.tensor_tensor(kb_first[:, 0:2], kb_parts[:, 0:2, 0], kb_parts[:, 0:2, 1], ADD)
-        nc.gpsimd.tensor_tensor(kb_mid[:, 2:7], kb_parts[:, 2:7, 0], kb_parts[:, 2:7, 1], ADD)
-        nc.gpsimd.tensor_tensor(kb_last[:, 7:8], kb_parts[:, 7:8, 0], kb_parts[:, 7:8, 1], ADD)
-        gather_keys_plain(1)
-        for g in range(PASSES):
-            interleave_keys(g)
-        vs_parts = columns(vs_row, VS_PART, "vs")
-        vs_cols = keep.tile([P, PASSES * PACK], F32, name="vs_cols")
-        nc.gpsimd.tensor_tensor(vs_cols[:], vs_parts[:, :, 0], vs_parts[:, :, 1], ADD)
+        def columns(row, first, target, first_bank, name):
+            for g in range(PASSES):
+                picked = keep.tile([P, PASS], F32, name="%s_picked%d" % (name, g))
+                gather(g, picked[:], row)
+                turned = bank(first_bank + g, [P, PACK, P], "%s_turned%d" % (name, g))
+                for t in range(PACK):
+                    nc.tensor.transpose(turned[:, t, :], picked[:, t:PASS:PACK], ident[:])
+                nc.vector.tensor_reduce(
+                    target[:, PACK * g : PACK * (g + 1)], turned[:, :, first:P:PIECE_STEP], axis=X, op=ADD
+                )
+
+        kb_cols = tail.tile([P, PASSES * PACK], F32, name="kb_cols", align_bytes=64, offset=0)
         vs_wide = keep.tile([P, P], F32, name="vs_wide")
         nc.gpsimd.memset(vs_wide[:, PASSES * PACK : P], 0.0)
-        nc.gpsimd.tensor_copy(vs_wide[:, 0 : PASSES * PACK], vs_cols[:])
-        vs_there = turn_psum.tile([P, P], F32, name="vs_there", tag="turned")
+
+        gather_keys(0)
+        columns(kb_row, KB_PART, kb_cols, 0, "kb")
+        gather_keys(1)
+        columns(vs_row, VS_PART, vs_wide, 2, "vs")
+        vs_there = bank(4, [P, P], "vs_there")
         nc.tensor.transpose(vs_there[:], vs_wide[:], ident[:])
         vs_turned = keep.tile([P, P], F32, name="vs_turned")
         nc.scalar.copy(vs_turned[:], vs_there[:])
-        vs_back = y_psum.tile([P, P], F32, name="vs_back", tag="y")
+        vs_back = bank(7, [P, P], "vs_back")
         nc.tensor.transpose(vs_back[:], vs_turned[:], ident[:])
-        gather_keys_half(2, 0)
-        gather_keys_half(2, 1)
-        q_packed = tail.tile([P, QUERIES, PACK], BF16, name="q_packed", align_bytes=64, offset=15424)
+        gather_keys(2)
+
+        q_packed = k_second[:, 0, 2:4, :, :].rearrange("p b c j -> p (b c) j")
         q_codes = keep.tile([P, QUERIES], U32, name="q_codes", align_bytes=64)
         q_scales = keep.tile([P, QUERIES], U8, name="q_scales", align_bytes=64)
-        nc.scalar.copy(
-            q_packed[:].rearrange("p (b c i) j -> p c j i b", b=Q_BLOCKS, i=RUN // Q_BLOCKS),
-            q_raw[:].rearrange("p j (c i b) -> p c j i b", b=Q_BLOCKS, i=RUN // Q_BLOCKS),
-        )
 
-        k_codes = {}
-
-        def quantize_keys(g, t0, t1, pool, **place):
-            codes = pool.tile([P, P * (t1 - t0)], U32, name="k_codes%d_%d" % (g, t0), align_bytes=64, **place)
-            for t in range(t0, t1):
-                k_codes[g, t] = codes[:, P * (t - t0) : P * (t - t0 + 1)]
-            nc.vector.quantize_mx(
-                out=codes[:].bitcast(FP8X4),
-                scales=k_scales[:, PASS * g + P * t0 : PASS * g + P * t1],
-                in_=k_packed[g, t0 // 2][:, t0 % 2 : t0 % 2 + t1 - t0, :, :].rearrange("p t m j -> p (t m j)"),
+        def gather_last_keys(rows):
+            first = (PASS + PACK * rows.start) // 16
+            last = (PASS + PACK * rows.stop) // 16
+            nc.scalar.activation(
+                k_packed[1][:, :, :, rows, PACK - 1].rearrange("p u e m -> p m u e"),
+                k_planes[PACK - 1][:].indirect(offsets[:, first:last]),
+                COPY,
             )
 
-        p_tiles = [keep.tile([P, PACK, QUERIES], F32, name="p_tile%d" % g, tag="p%d" % g, align_bytes=64) for g in range(PASSES)]
-        v_first = tail.tile([P, PASS], BF16, name="v_first", align_bytes=64, offset=4096)
-        v_second = tail.tile([P, PASS], BF16, name="v_second", align_bytes=64, offset=4096 + 1600)
-        v_tiles = [half.tile([P, V_FEATURES, PACK], BF16, name="v_packed%d" % g, align_bytes=64) for g in range(PASSES)]
-        w_codes = []
-        w_scales = keep.tile([P, PASSES, QUERIES], U8, name="w_scales", align_bytes=64)
-        v_codes = []
-        v_scales = keep.tile([P, PASSES, V_FEATURES], U8, name="v_scales", align_bytes=64)
+        def interleave_queries(copy, runs):
+            copy(
+                q_packed.rearrange("p (b c i) j -> p c j i b", b=Q_BLOCKS, i=RUN // Q_BLOCKS)[:, runs],
+                q_raw[:].rearrange("p j (c i b) -> p c j i b", b=Q_BLOCKS, i=RUN // Q_BLOCKS)[:, runs],
+            )
 
-        def score(g, places):
-            for t in places:
-                bank = score_psum.tile([P, QUERIES], F32, name="bank")
-                nc.tensor.matmul_mx(
-                    out=bank[:],
-                    lhsT=k_codes[g, t].bitcast(FP8X4),
-                    lhsT_scale=k_scales[:, PASS * g + P * t : PASS * g + P * (t + 1)],
-                    rhs=q_codes[:].bitcast(FP8X4),
-                    rhs_scale=q_scales[:],
-                    start=True,
-                    stop=True,
+        gather(0, k_packed[0][:, :, :, :, PACK - 1].rearrange("p u e m -> p m u e"), k_planes[PACK - 1])
+        gather_last_keys(slice(0, EARLY_ROWS))
+        interleave_queries(nc.vector.tensor_copy, slice(0, Q_SPLIT))
+        interleave_queries(nc.scalar.copy, slice(Q_SPLIT, QUERIES // RUN))
+        nc.vector.quantize_mx(
+            out=q_codes[:].bitcast(FP8X4), scales=q_scales[:], in_=q_packed.rearrange("p q j -> p (q j)")
+        )
+        gather_last_keys(slice(EARLY_ROWS, P))
+
+        k_codes = keep.tile([P, SLOTS], U32, name="k_codes", align_bytes=64)
+        k_scales = keep.tile([P, SLOTS], U8, name="k_scales", align_bytes=64)
+
+        def quantize_keys(g, t0, t1):
+            cols = slice(PASS * g + P * t0, PASS * g + P * t1)
+            nc.vector.quantize_mx(
+                out=k_codes[:, cols].bitcast(FP8X4),
+                scales=k_scales[:, cols],
+                in_=k_packed[g][:, t0 // 2, t0 % 2 : t0 % 2 + t1 - t0, :, :].rearrange("p t m j -> p (t m j)"),
+            )
+
+        def score(g, t):
+            cols = slice(PASS * g + P * t, PASS * g + P * (t + 1))
+            scores = bank((PACK * g + t) % 7, [P, QUERIES], "scores%d%d" % (g, t))
+            nc.tensor.matmul_mx(
+                out=scores[:],
+                lhsT=k_codes[:, cols].bitcast(FP8X4),
+                lhsT_scale=k_scales[:, cols],
+                rhs=q_codes[:].bitcast(FP8X4),
+                rhs_scale=q_scales[:],
+                start=True,
+                stop=True,
+            )
+            return scores
+
+        quantize_keys(0, 0, 1)
+        quantize_keys(0, 1, 2)
+        quantize_keys(0, 2, 4)
+        quantize_keys(1, 0, 2)
+        quantize_keys(1, 2, 4)
+
+        p_early = tail.tile([P, PACK, P], F32, name="p_early", align_bytes=64, offset=1024)
+        p_next = keep.tile([P, PACK, P], F32, name="p_next")
+        p_last = tail.tile([P, PACK, QUERIES], F32, name="p_last", align_bytes=64, offset=12288)
+        first_scores = [score(0, t) for t in range(PACK)]
+        for b, p_tile in enumerate((p_early, p_next)):
+            for t in range(PACK):
+                nc.scalar.activation(
+                    p_tile[:, t, :], first_scores[t][:, P * b : P * (b + 1)], SILU, bias=kb_cols[:, t : t + 1]
                 )
-                col = PACK * g + t
-                biases = kb_first if col < 2 else kb_mid if col < 7 else kb_last
-                nc.scalar.activation(p_tiles[g][:, t, :], bank[:], SILU, bias=biases[:, col : col + 1])
+        for t in range(PACK):
+            nc.scalar.activation(p_last[:, t, :], score(1, t)[:], SILU, bias=kb_cols[:, PACK + t : PACK + t + 1])
 
-        w_first = tail.tile([P, QUERIES, PACK], BF16, name="w_first", align_bytes=64, offset=1024)
-        w_own = tail.tile([P, P, PACK], BF16, name="w_own", align_bytes=64, offset=4096 - 960)
-        w_shared = tail.tile([P, P, PACK], BF16, name="w_shared", align_bytes=64, offset=0)
-        pairs_first = keep.tile([P, 2, QUERIES, 2], BF16, name="w_pairs")
+        around = tail.tile([P, 2, PASS // 2 + (QUERIES - SHARE) * PACK], BF16, name="around", align_bytes=64, offset=1024)
+        w_first = keep.tile([P, QUERIES, PACK], BF16, name="w_first", align_bytes=64)
+        w_own = around[:, 0, PASS // 2 :].rearrange("p (q t) -> p q t", t=PACK)
+        w_shared = keep.tile([P, SHARE, PACK], BF16, name="w_shared", align_bytes=64)
 
-        def weigh(engine, target, g, q_cols, places, scales):
-            count = places.stop - places.start
-            width = q_cols.stop - q_cols.start
+        def weigh(engine, g, target, source, scales):
+            width = target.shape[1]
             engine.tensor_tensor(
                 target.rearrange("p (c i) t -> p c t i", i=RUN),
-                p_tiles[g][:, places, q_cols].rearrange("p t (c i) -> p c t i", i=RUN),
-                scales[:, PACK * g + places.start : PACK * g + places.stop]
-                .unsqueeze(1)
-                .unsqueeze(3)
-                .to_broadcast([P, width // RUN, count, RUN]),
+                source.rearrange("p t (c i) -> p c t i", i=RUN),
+                scales[:, PACK * g : PACK * (g + 1)].unsqueeze(1).unsqueeze(3).to_broadcast([P, width // RUN, PACK, RUN]),
                 MULT,
             )
 
-        def weave_first():
-            nc.scalar.copy(
-                w_first[:].rearrange("p q t -> p (q t)").bitcast(F32).rearrange("p (q u) -> p q u", u=2),
-                pairs_first[:].rearrange("p u q e -> p u (q e)").bitcast(F32).rearrange("p u q -> p q u"),
-            )
+        v_second = tail.tile([P, 2, PASS // 2], BF16, name="v_second", align_bytes=64, offset=0)
+        v_picked = [around[:, :, 0 : PASS // 2], v_second[:]]
+        v_packed = [keep.tile([P, V_FEATURES, PACK], BF16, name="v_packed%d" % g, align_bytes=64) for g in range(PASSES)]
 
-        def quantize_weights(g, q_cols, source):
-            if len(w_codes) == g:
-                if g == 0:
-                    w_codes.append(tail.tile([P, QUERIES], U32, name="w_codes0", align_bytes=64, offset=4096 + 576))
-                else:
-                    w_codes.append(keep.tile([P, QUERIES], U32, name="w_codes1", tag="p1", align_bytes=64))
-            nc.vector.quantize_mx(
-                out=w_codes[g][:, q_cols].bitcast(FP8X4),
-                scales=w_scales[:, g, q_cols],
-                in_=source.rearrange("p q t -> p (q t)"),
-            )
-
-        def gather_values(g):
-            v_picked = v_first[:] if g == 0 else v_second[:]
-            nc.vector.tensor_copy(
-                v_picked.rearrange("p (u m e) -> p m u e", u=2, e=2),
-                v_pool[:].indirect(offsets[:, 32 * g : 32 * g + 32]),
-            )
-            pairs = v_picked.bitcast(F32)
-            turned = turn_psum.tile([P, 2, P], F32, name="turned_v", tag="turned")
+        def turn_values(g):
+            turned = bank(g, [P, 2, P], "v_turned%d" % g)
             for u in range(2):
-                nc.tensor.transpose(turned[:, u, :], pairs[:, P * u : P * (u + 1)], ident[:])
+                nc.tensor.transpose(turned[:, u, :], v_picked[g][:, u, :].bitcast(F32), ident[:])
             nc.scalar.copy(
-                v_tiles[g][:].rearrange("p e t -> p (e t)").bitcast(F32).rearrange("p (e u) -> p e u", u=2),
+                v_packed[g][:].rearrange("p e t -> p (e t)").bitcast(F32).rearrange("p (e u) -> p e u", u=2),
                 turned[:].rearrange("p u e -> p e u"),
             )
 
-        def quantize_values(g):
-            if g == 0:
-                v_codes.append(tail.tile([P, V_FEATURES], U32, name="v_codes0", align_bytes=64, offset=4096 + 64))
-            else:
-                v_codes.append(tail.tile([P, V_FEATURES], U32, name="v_codes1", align_bytes=64, offset=1024))
-            nc.vector.quantize_mx(
-                out=v_codes[g][:].bitcast(FP8X4),
-                scales=v_scales[:, g, :],
-                in_=v_tiles[g][:].rearrange("p e t -> p (e t)"),
-            )
+        own = slice(0, QUERIES - SHARE)
+        shared = slice(QUERIES - SHARE, QUERIES)
+        weigh(nc.vector, 0, w_first[:, 0:P, :], p_early[:], vs_back)
+        weigh(nc.gpsimd, 0, w_first[:, P:QUERIES, :], p_next[:], vs_wide)
+        for g in range(PASSES):
+            gather(g, v_picked[g].rearrange("p u (m e) -> p m u e", e=2), v_pool)
+        for g in range(PASSES):
+            turn_values(g)
+        weigh(nc.vector, 1, w_own, p_last[:, :, own], vs_back)
+        weigh(nc.gpsimd, 1, w_shared[:], p_last[:, :, shared], vs_wide)
 
-        gather_keys_half(3, 0)
-        gather_keys_half(3, 1)
-        weave_keys(nc.vector.tensor_copy, 0, 0)
-        weave_keys(nc.scalar.copy, 1, 0)
-        weave_keys(nc.scalar.copy, 1, 1)
-        nc.vector.quantize_mx(
-            out=q_codes[:].bitcast(FP8X4), scales=q_scales[:], in_=q_packed[:].rearrange("p q j -> p (q j)")
-        )
-        quantize_keys(0, 0, 1, tail, offset=10304)
-        quantize_keys(0, 1, 2, tail, offset=10816)
-        weave_keys(nc.vector.tensor_copy, 0, 1)
-        quantize_keys(1, 0, 2, keep)
-        quantize_keys(0, 2, 4, keep)
-        quantize_keys(1, 2, 4, keep)
-        score(0, range(0, 2))
-        score(1, range(0, 1))
-        score(0, range(2, PACK))
-        score(1, range(1, PACK))
-        weigh(nc.vector, pairs_first[:, 0, :, :], 0, slice(0, QUERIES), slice(0, 2), vs_back)
-        for t in range(2, PACK):
-            nc.gpsimd.tensor_scalar(
-                pairs_first[:, 1, :, t % 2], p_tiles[0][:, t, :], vs_cols[:, t : t + 1], 0.0, MULT, ADD
-            )
-        weigh(nc.gpsimd, w_shared[:, SHARE:P, :], 1, slice(P + SHARE, QUERIES), slice(0, PACK), vs_cols)
-        for t in range(PACK):
-            nc.scalar.activation(
-                w_shared[:, 0:SHARE, t], p_tiles[1][:, t, P : P + SHARE], COPY, scale=vs_cols[:, PACK + t : PACK + t + 1]
-            )
-        weave_first()
-        gather_values(0)
-        gather_values(1)
-        weigh(nc.vector, w_own[:], 1, slice(0, P), slice(0, PACK), vs_back)
-        quantize_weights(0, slice(0, QUERIES), w_first[:])
-        quantize_values(0)
-        quantize_weights(1, slice(0, P), w_own[:])
-        quantize_values(1)
-        quantize_weights(1, slice(P, QUERIES), w_shared[:])
+        w_codes = [
+            tail.tile([P, QUERIES], U32, name="w_codes%d" % g, align_bytes=64, offset=12288 + 1024 * g)
+            for g in range(PASSES)
+        ]
+        v_codes = [
+            tail.tile([P, V_FEATURES], U32, name="v_codes%d" % g, align_bytes=64, offset=14336 + 512 * g)
+            for g in range(PASSES)
+        ]
+        w_scales = keep.tile([P, PASSES, QUERIES], U8, name="w_scales", align_bytes=64)
+        v_scales = keep.tile([P, PASSES, V_FEATURES], U8, name="v_scales", align_bytes=64)
+
+        def quantize(codes, scales, source):
+            nc.vector.quantize_mx(out=codes.bitcast(FP8X4), scales=scales, in_=source.rearrange("p x t -> p (x t)"))
+
+        rest = slice(P, QUERIES - SHARE)
+        quantize(w_codes[0][:], w_scales[:, 0, :], w_first[:])
+        quantize(v_codes[0][:], v_scales[:, 0, :], v_packed[0][:])
+        quantize(w_codes[1][:, 0:P], w_scales[:, 1, 0:P], w_own[:, 0:P, :])
+        quantize(w_codes[1][:, rest], w_scales[:, 1, rest], w_own[:, rest, :])
+        quantize(w_codes[1][:, shared], w_scales[:, 1, shared], w_shared[:])
+        quantize(v_codes[1][:], v_scales[:, 1, :], v_packed[1][:])
 
         for b in range(Q_BLOCKS):
             q_cols = slice(P * b, P * (b + 1))
-            y = y_psum.tile([P, V_FEATURES], F32, name="y", tag="y")
+            y = bank(2 + b, [P, V_FEATURES], "y%d" % b)
             for g in range(PASSES):
                 nc.tensor.matmul_mx(
                     out=y[:],
@@ -314,7 +276,7 @@ def tile_attend_silu_gate_kernel(tc, qT, kT, vT, vs, kb, og, offs, out):
                     start=(g == 0),
                     stop=(g == PASSES - 1),
                 )
-            result = half.tile([P, V_FEATURES], F32, name="result")
+            result = keep.tile([P, V_FEATURES], F32, name="result%d" % b)
             nc.vector.scalar_tensor_tensor(result[:], y[:], 1.0 / 16.0, gate[:, b, :], MULT, MULT)
             queue = nc.scalar if b == 0 else nc.sync
             queue.dma_start(out[0].rearrange("(p b) e -> b p e", b=Q_BLOCKS)[b], result[:])

@@ -37,8 +37,7 @@ PIECE_STEP = 64
 KB_PART = 0
 VS_PART = 4
 SHARE = 64
-EARLY_ROWS = 80
-Q_SPLIT = 40
+HALF = 64
 
 
 def tile_attend_silu_gate_kernel(tc, qT, kT, vT, vs, kb, og, offs, out):
@@ -57,7 +56,7 @@ def tile_attend_silu_gate_kernel(tc, qT, kT, vT, vs, kb, og, offs, out):
         vs_row = keep.tile([P, TOKENS], F32, name="vs_row")
         k_planes = [keep.tile([P, TOKENS], F32, name="k_plane%d" % j) for j in range(PACK)]
         v_pool = keep.tile([P, TOKENS], F32, name="v_pool")
-        q_raw = keep.tile([P, PACK, QUERIES], F32, name="q_raw")
+        q_raw = keep.tile([P, PACK, QUERIES], F32, name="q_raw", align_bytes=64)
         gate_in = tail.tile([P, Q_BLOCKS, V_FEATURES], F32, name="gate_in", align_bytes=64, offset=8192)
 
         k_rows = kT.rearrange("(p j) n -> j p n", j=PACK)
@@ -65,7 +64,7 @@ def tile_attend_silu_gate_kernel(tc, qT, kT, vT, vs, kb, og, offs, out):
         for row in (kb_row, vs_row):
             nc.vector.memset(row[:].bitcast(I32), 0)
         make_identity(nc, ident[:])
-        nc.scalar.dma_start(gate_in[:], og[0].rearrange("(p b) e -> p b e", b=Q_BLOCKS))
+        nc.scalar.dma_start(gate_in[:], og[0].rearrange("(b p) e -> p b e", b=Q_BLOCKS))
 
         def load_row(row, source, first):
             for piece in range(PIECES):
@@ -97,9 +96,9 @@ def tile_attend_silu_gate_kernel(tc, qT, kT, vT, vs, kb, og, offs, out):
             else:
                 nc.scalar.activation(target, picked, COPY)
 
-        k_first = keep.tile([P, 2, 2, P, PACK], BF16, name="k_first", align_bytes=64)
-        k_second = keep.tile([P, 2, 4, P, PACK], BF16, name="k_second", align_bytes=64)
-        k_packed = [k_first[:], k_second[:, :, 0:2, :, :]]
+        k_first = keep.tile([P, 2, HALF + PASS, PACK], BF16, name="k_first", align_bytes=64)
+        k_second = keep.tile([P, 2, 2, P, PACK], BF16, name="k_second", align_bytes=64)
+        k_packed = [k_first[:, 0, HALF:, :].rearrange("p (u e m) j -> p u e m j", u=2, e=2), k_second[:]]
 
         def gather_keys(j):
             for g in range(PASSES):
@@ -132,78 +131,77 @@ def tile_attend_silu_gate_kernel(tc, qT, kT, vT, vs, kb, og, offs, out):
         nc.tensor.transpose(vs_back[:], vs_turned[:], ident[:])
         gather_keys(2)
 
-        q_packed = k_second[:, 0, 2:4, :, :].rearrange("p b c j -> p (b c) j")
+        q_first = k_first[:, :, 0:HALF, :]
+        q_second = tail.tile([P, P, PACK], BF16, name="q_second", align_bytes=64, offset=20480)
         q_codes = keep.tile([P, QUERIES], U32, name="q_codes", align_bytes=64)
         q_scales = keep.tile([P, QUERIES], U8, name="q_scales", align_bytes=64)
 
-        def gather_last_keys(rows):
-            first = (PASS + PACK * rows.start) // 16
-            last = (PASS + PACK * rows.stop) // 16
-            nc.scalar.activation(
-                k_packed[1][:, :, :, rows, PACK - 1].rearrange("p u e m -> p m u e"),
-                k_planes[PACK - 1][:].indirect(offsets[:, first:last]),
-                COPY,
-            )
+        def quantize(codes, scales, source):
+            nc.vector.quantize_mx(out=codes.bitcast(FP8X4), scales=scales, in_=source.rearrange("p x t -> p (x t)"))
 
-        def interleave_queries(copy, runs):
-            copy(
-                q_packed.rearrange("p (b c i) j -> p c j i b", b=Q_BLOCKS, i=RUN // Q_BLOCKS)[:, runs],
-                q_raw[:].rearrange("p j (c i b) -> p c j i b", b=Q_BLOCKS, i=RUN // Q_BLOCKS)[:, runs],
-            )
+        def quantize_queries(first, last, source):
+            quantize(q_codes[:, first:last], q_scales[:, first:last], source)
 
-        gather(0, k_packed[0][:, :, :, :, PACK - 1].rearrange("p u e m -> p m u e"), k_planes[PACK - 1])
-        gather_last_keys(slice(0, EARLY_ROWS))
-        interleave_queries(nc.vector.tensor_copy, slice(0, Q_SPLIT))
-        interleave_queries(nc.scalar.copy, slice(Q_SPLIT, QUERIES // RUN))
-        nc.vector.quantize_mx(
-            out=q_codes[:].bitcast(FP8X4), scales=q_scales[:], in_=q_packed.rearrange("p q j -> p (q j)")
+        gather_keys(3)
+        nc.vector.tensor_copy(
+            q_first.rearrange("p h (c i) j -> p h c j i", i=RUN),
+            q_raw[:, :, 0:P].rearrange("p j (h c i) -> p h c j i", h=2, i=RUN),
         )
-        gather_last_keys(slice(EARLY_ROWS, P))
+        nc.scalar.copy(
+            q_second[:].rearrange("p (c i) j -> p c j i", i=RUN),
+            q_raw[:, :, P:QUERIES].rearrange("p j (c i) -> p c j i", i=RUN),
+        )
 
-        k_codes = keep.tile([P, SLOTS], U32, name="k_codes", align_bytes=64)
+        k_codes = [
+            keep.tile([P, PASS], U32, name="k_codes0", align_bytes=64),
+            tail.tile([P, PASS], U32, name="k_codes1", align_bytes=64, offset=20480),
+        ]
         k_scales = keep.tile([P, SLOTS], U8, name="k_scales", align_bytes=64)
 
         def quantize_keys(g, t0, t1):
-            cols = slice(PASS * g + P * t0, PASS * g + P * t1)
-            nc.vector.quantize_mx(
-                out=k_codes[:, cols].bitcast(FP8X4),
-                scales=k_scales[:, cols],
-                in_=k_packed[g][:, t0 // 2, t0 % 2 : t0 % 2 + t1 - t0, :, :].rearrange("p t m j -> p (t m j)"),
+            first, last = PASS * g + P * t0, PASS * g + P * t1
+            quantize(
+                k_codes[g][:, P * t0 : P * t1],
+                k_scales[:, first:last],
+                k_packed[g][:, t0 // 2, t0 % 2 : t0 % 2 + t1 - t0, :, :].rearrange("p t m j -> p (t m) j"),
             )
 
-        def score(g, t):
-            cols = slice(PASS * g + P * t, PASS * g + P * (t + 1))
-            scores = bank((PACK * g + t) % 7, [P, QUERIES], "scores%d%d" % (g, t))
+        def score(index, g, t, q_cols):
+            first, last = PASS * g + P * t, PASS * g + P * (t + 1)
+            scores = bank(index % 7, [P, q_cols.stop - q_cols.start], "scores%d" % index)
             nc.tensor.matmul_mx(
                 out=scores[:],
-                lhsT=k_codes[:, cols].bitcast(FP8X4),
-                lhsT_scale=k_scales[:, cols],
-                rhs=q_codes[:].bitcast(FP8X4),
-                rhs_scale=q_scales[:],
+                lhsT=k_codes[g][:, P * t : P * (t + 1)].bitcast(FP8X4),
+                lhsT_scale=k_scales[:, first:last],
+                rhs=q_codes[:, q_cols].bitcast(FP8X4),
+                rhs_scale=q_scales[:, q_cols],
                 start=True,
                 stop=True,
             )
-            return scores
+            return scores[:]
 
         quantize_keys(0, 0, 1)
+        for h in range(2):
+            quantize_queries(HALF * h, HALF * (h + 1), q_first[:, h, :, :])
         quantize_keys(0, 1, 2)
         quantize_keys(0, 2, 4)
+        quantize_queries(P, QUERIES, q_second[:])
         quantize_keys(1, 0, 2)
         quantize_keys(1, 2, 4)
 
-        p_early = tail.tile([P, PACK, P], F32, name="p_early", align_bytes=64, offset=1024)
-        p_next = keep.tile([P, PACK, P], F32, name="p_next")
+        p_first = [keep.tile([P, PACK, P], F32, name="p_first%d" % b) for b in range(Q_BLOCKS)]
         p_last = tail.tile([P, PACK, QUERIES], F32, name="p_last", align_bytes=64, offset=12288)
-        first_scores = [score(0, t) for t in range(PACK)]
-        for b, p_tile in enumerate((p_early, p_next)):
+        for b in range(Q_BLOCKS):
             for t in range(PACK):
-                nc.scalar.activation(
-                    p_tile[:, t, :], first_scores[t][:, P * b : P * (b + 1)], SILU, bias=kb_cols[:, t : t + 1]
-                )
+                scores = score(PACK * b + t, 0, t, slice(P * b, P * (b + 1)))
+                nc.scalar.activation(p_first[b][:, t, :], scores, SILU, bias=kb_cols[:, t : t + 1])
         for t in range(PACK):
-            nc.scalar.activation(p_last[:, t, :], score(1, t)[:], SILU, bias=kb_cols[:, PACK + t : PACK + t + 1])
+            scores = score(2 * PACK + t, 1, t, slice(0, QUERIES))
+            nc.scalar.activation(p_last[:, t, :], scores, SILU, bias=kb_cols[:, PACK + t : PACK + t + 1])
 
-        around = tail.tile([P, 2, PASS // 2 + (QUERIES - SHARE) * PACK], BF16, name="around", align_bytes=64, offset=1024)
+        around = keep.tile([P, 2, PASS // 2 + (QUERIES - SHARE) * PACK], BF16, name="around", align_bytes=64)
+        v_second = keep.tile([P, 2, PASS // 2], BF16, name="v_second", align_bytes=64)
+        v_picked = [around[:, :, 0 : PASS // 2], v_second[:]]
         w_first = keep.tile([P, QUERIES, PACK], BF16, name="w_first", align_bytes=64)
         w_own = around[:, 0, PASS // 2 :].rearrange("p (q t) -> p q t", t=PACK)
         w_shared = keep.tile([P, SHARE, PACK], BF16, name="w_shared", align_bytes=64)
@@ -217,12 +215,10 @@ def tile_attend_silu_gate_kernel(tc, qT, kT, vT, vs, kb, og, offs, out):
                 MULT,
             )
 
-        v_second = tail.tile([P, 2, PASS // 2], BF16, name="v_second", align_bytes=64, offset=0)
-        v_picked = [around[:, :, 0 : PASS // 2], v_second[:]]
         v_packed = [keep.tile([P, V_FEATURES, PACK], BF16, name="v_packed%d" % g, align_bytes=64) for g in range(PASSES)]
 
         def turn_values(g):
-            turned = bank(g, [P, 2, P], "v_turned%d" % g)
+            turned = bank(5 + g, [P, 2, P], "v_turned%d" % g)
             for u in range(2):
                 nc.tensor.transpose(turned[:, u, :], v_picked[g][:, u, :].bitcast(F32), ident[:])
             nc.scalar.copy(
@@ -230,20 +226,15 @@ def tile_attend_silu_gate_kernel(tc, qT, kT, vT, vs, kb, og, offs, out):
                 turned[:].rearrange("p u e -> p e u"),
             )
 
-        own = slice(0, QUERIES - SHARE)
-        shared = slice(QUERIES - SHARE, QUERIES)
-        weigh(nc.vector, 0, w_first[:, 0:P, :], p_early[:], vs_back)
-        weigh(nc.gpsimd, 0, w_first[:, P:QUERIES, :], p_next[:], vs_wide)
-        for g in range(PASSES):
-            gather(g, v_picked[g].rearrange("p u (m e) -> p m u e", e=2), v_pool)
-        for g in range(PASSES):
-            turn_values(g)
-        weigh(nc.vector, 1, w_own, p_last[:, :, own], vs_back)
-        weigh(nc.gpsimd, 1, w_shared[:], p_last[:, :, shared], vs_wide)
-
         w_codes = [
-            tail.tile([P, QUERIES], U32, name="w_codes%d" % g, align_bytes=64, offset=12288 + 1024 * g)
-            for g in range(PASSES)
+            [
+                keep.tile([P, P], U32, name="w_codes00", align_bytes=64),
+                tail.tile([P, P], U32, name="w_codes01", align_bytes=64, offset=13312),
+            ],
+            [
+                tail.tile([P, P], U32, name="w_codes10", align_bytes=64, offset=12288),
+                tail.tile([P, P], U32, name="w_codes11", align_bytes=64, offset=12800),
+            ],
         ]
         v_codes = [
             tail.tile([P, V_FEATURES], U32, name="v_codes%d" % g, align_bytes=64, offset=14336 + 512 * g)
@@ -252,24 +243,32 @@ def tile_attend_silu_gate_kernel(tc, qT, kT, vT, vs, kb, og, offs, out):
         w_scales = keep.tile([P, PASSES, QUERIES], U8, name="w_scales", align_bytes=64)
         v_scales = keep.tile([P, PASSES, V_FEATURES], U8, name="v_scales", align_bytes=64)
 
-        def quantize(codes, scales, source):
-            nc.vector.quantize_mx(out=codes.bitcast(FP8X4), scales=scales, in_=source.rearrange("p x t -> p (x t)"))
-
+        own = slice(0, QUERIES - SHARE)
+        shared = slice(QUERIES - SHARE, QUERIES)
         rest = slice(P, QUERIES - SHARE)
-        quantize(w_codes[0][:], w_scales[:, 0, :], w_first[:])
+        for b in range(Q_BLOCKS):
+            weigh(nc.vector, 0, w_first[:, P * b : P * (b + 1), :], p_first[b][:], vs_back)
+        quantize(w_codes[0][0][:], w_scales[:, 0, 0:P], w_first[:, 0:P, :])
+        weigh(nc.gpsimd, 1, w_shared[:], p_last[:, :, shared], vs_wide)
+        for g in range(PASSES):
+            gather(g, v_picked[g].rearrange("p u (m e) -> p m u e", e=2), v_pool)
+        for g in range(PASSES):
+            turn_values(g)
+        weigh(nc.vector, 1, w_own, p_last[:, :, own], vs_back)
+        quantize(w_codes[0][1][:], w_scales[:, 0, P:QUERIES], w_first[:, P:QUERIES, :])
         quantize(v_codes[0][:], v_scales[:, 0, :], v_packed[0][:])
-        quantize(w_codes[1][:, 0:P], w_scales[:, 1, 0:P], w_own[:, 0:P, :])
-        quantize(w_codes[1][:, rest], w_scales[:, 1, rest], w_own[:, rest, :])
-        quantize(w_codes[1][:, shared], w_scales[:, 1, shared], w_shared[:])
+        quantize(w_codes[1][0][:], w_scales[:, 1, 0:P], w_own[:, 0:P, :])
+        quantize(w_codes[1][1][:, 0 : P - SHARE], w_scales[:, 1, rest], w_own[:, rest, :])
+        quantize(w_codes[1][1][:, P - SHARE : P], w_scales[:, 1, shared], w_shared[:])
         quantize(v_codes[1][:], v_scales[:, 1, :], v_packed[1][:])
 
         for b in range(Q_BLOCKS):
             q_cols = slice(P * b, P * (b + 1))
-            y = bank(2 + b, [P, V_FEATURES], "y%d" % b)
+            y = bank(b, [P, V_FEATURES], "y%d" % b)
             for g in range(PASSES):
                 nc.tensor.matmul_mx(
                     out=y[:],
-                    lhsT=w_codes[g][:, q_cols].bitcast(FP8X4),
+                    lhsT=w_codes[g][b][:].bitcast(FP8X4),
                     lhsT_scale=w_scales[:, g, q_cols],
                     rhs=v_codes[g][:].bitcast(FP8X4),
                     rhs_scale=v_scales[:, g, :],
@@ -279,4 +278,4 @@ def tile_attend_silu_gate_kernel(tc, qT, kT, vT, vs, kb, og, offs, out):
             result = keep.tile([P, V_FEATURES], F32, name="result%d" % b)
             nc.vector.scalar_tensor_tensor(result[:], y[:], 1.0 / 16.0, gate[:, b, :], MULT, MULT)
             queue = nc.scalar if b == 0 else nc.sync
-            queue.dma_start(out[0].rearrange("(p b) e -> b p e", b=Q_BLOCKS)[b], result[:])
+            queue.dma_start(out[0, q_cols, :], result[:])

@@ -36,7 +36,7 @@ PIECES = 2
 PIECE_STEP = 64
 KB_PART = 0
 VS_PART = 4
-SHARE = 64
+SHARE = 128
 HALF = 64
 
 
@@ -245,7 +245,6 @@ def tile_attend_silu_gate_kernel(tc, qT, kT, vT, vs, kb, og, offs, out):
 
         own = slice(0, QUERIES - SHARE)
         shared = slice(QUERIES - SHARE, QUERIES)
-        rest = slice(P, QUERIES - SHARE)
         for b in range(Q_BLOCKS):
             weigh(nc.vector, 0, w_first[:, P * b : P * (b + 1), :], p_first[b][:], vs_back)
         quantize(w_codes[0][0][:], w_scales[:, 0, 0:P], w_first[:, 0:P, :])
@@ -258,9 +257,8 @@ def tile_attend_silu_gate_kernel(tc, qT, kT, vT, vs, kb, og, offs, out):
         quantize(w_codes[0][1][:], w_scales[:, 0, P:QUERIES], w_first[:, P:QUERIES, :])
         quantize(v_codes[0][:], v_scales[:, 0, :], v_packed[0][:])
         quantize(w_codes[1][0][:], w_scales[:, 1, 0:P], w_own[:, 0:P, :])
-        quantize(w_codes[1][1][:, 0 : P - SHARE], w_scales[:, 1, rest], w_own[:, rest, :])
-        quantize(w_codes[1][1][:, P - SHARE : P], w_scales[:, 1, shared], w_shared[:])
         quantize(v_codes[1][:], v_scales[:, 1, :], v_packed[1][:])
+        quantize(w_codes[1][1][:], w_scales[:, 1, shared], w_shared[:])
 
         for b in range(Q_BLOCKS):
             q_cols = slice(P * b, P * (b + 1))

from contextlib import ExitStack

import concourse.mybir as mybir
from concourse.masks import make_identity

QUERIES = 256
FEATURES = 512
SLOTS = 1024
TOKENS = 4096
V_FEATURES = 128

FLOPS = 2 * QUERIES * SLOTS * (FEATURES + V_FEATURES)

F32 = mybir.dt.float32
BF16 = mybir.dt.bfloat16
U32 = mybir.dt.uint32
I32 = mybir.dt.int32
U16 = mybir.dt.uint16
U8 = mybir.dt.uint8
FP8X4 = mybir.dt.float8_e4m3fn_x4

COPY = mybir.ActivationFunctionType.Copy
SIGMOID = mybir.ActivationFunctionType.Sigmoid
SILU = mybir.ActivationFunctionType.Silu
MULT = mybir.AluOpType.mult
ADD = mybir.AluOpType.add
X = mybir.AxisListType.X

P = 128
PACK = 4
PASS = P * PACK
PASSES = SLOTS // PASS
Q_BLOCKS = QUERIES // P
RUN = 4
PIECES = 2
PIECE_STEP = 64
KB_PART = 0
VS_PART = 4
SHARE = 128
HALF = 64


def tile_attend_silu_gate_kernel(tc, qT, kT, vT, vs, kb, og, offs, out):
    nc = tc.nc
    with ExitStack() as ctx:
        keep = ctx.enter_context(tc.tile_pool(name="keep", bufs=1))
        tail = ctx.enter_context(tc.tile_pool(name="tail", bufs=1))
        psum = ctx.enter_context(tc.psum_pool(name="psum", bufs=1))

        def bank(index, shape, name):
            return psum.tile(shape, F32, name=name, tag="bank%d" % index)

        offsets = keep.tile([P, SLOTS // 16], U16, name="offsets")
        ident = keep.tile([P, P], F32, name="ident")
        kb_row = keep.tile([P, TOKENS], F32, name="kb_row")
        vs_row = keep.tile([P, TOKENS], F32, name="vs_row")
        k_planes = [keep.tile([P, TOKENS], F32, name="k_plane%d" % j) for j in range(PACK)]
        v_pool = keep.tile([P, TOKENS], F32, name="v_pool")
        q_raw = keep.tile([P, PACK, QUERIES], F32, name="q_raw", align_bytes=64)
        gate_in = tail.tile([P, Q_BLOCKS, V_FEATURES], F32, name="gate_in", align_bytes=64, offset=8192)

        k_rows = kT.rearrange("(p j) n -> j p n", j=PACK)

        for row in (kb_row, vs_row):
            nc.vector.memset(row[:].bitcast(I32), 0)
        make_identity(nc, ident[:])
        nc.scalar.dma_start(gate_in[:], og[0].rearrange("(b p) e -> p b e", b=Q_BLOCKS))

        def load_row(row, source, first):
            for piece in range(PIECES):
                part = first + piece * PIECE_STEP
                tokens = slice(piece * TOKENS // PIECES, (piece + 1) * TOKENS // PIECES)
                nc.sync.dma_start(row[part : part + 1, tokens], source[part : part + 1, tokens])

        nc.sync.dma_start(k_planes[0][:], k_rows[0])
        nc.sync.dma_start(offsets[:], offs)
        load_row(kb_row, kb, KB_PART)
        nc.sync.dma_start(k_planes[1][:], k_rows[1])
        load_row(vs_row, vs, VS_PART)
        nc.sync.dma_start(k_planes[2][:], k_rows[2])
        nc.sync.dma_start(k_planes[3][:], k_rows[3])
        nc.sync.dma_start(q_raw[:], qT[0].rearrange("(p j) q -> p j q", j=PACK))
        nc.sync.dma_start(v_pool[:], vT)

        gate = keep.tile([P, Q_BLOCKS, V_FEATURES], F32, name="gate")
        nc.scalar.activation(gate[:], gate_in[:], SIGMOID)
        warm_in = keep.tile([P, 1], F32, name="warm_in")
        nc.gpsimd.memset(warm_in[:], 0.0)
        warm = tail.tile([P, 1], F32, name="warm", align_bytes=64, offset=8192)
        nc.scalar.activation(warm[:], warm_in[:], SILU)

        def gather(g, target, window):
            picked = window[:].indirect(offsets[:, 32 * g : 32 * g + 32])
            if g == 0:
                nc.vector.tensor_copy(target, picked)
            else:
                nc.scalar.activation(target, picked, COPY)

        k_first = keep.tile([P, 2, HALF + PASS, PACK], BF16, name="k_first", align_bytes=64)
        k_second = keep.tile([P, 2, 2, P, PACK], BF16, name="k_second", align_bytes=64)
        k_packed = [k_first[:, 0, HALF:, :].rearrange("p (u e m) j -> p u e m j", u=2, e=2), k_second[:]]

        def gather_keys(j):
            for g in range(PASSES):
                gather(g, k_packed[g][:, :, :, :, j].rearrange("p u e m -> p m u e"), k_planes[j])

        def columns(row, first, target, first_bank, name):
            for g in range(PASSES):
                picked = keep.tile([P, PASS], F32, name="%s_picked%d" % (name, g))
                gather(g, picked[:], row)
                turned = bank(first_bank + g, [P, PACK, P], "%s_turned%d" % (name, g))
                for t in range(PACK):
                    nc.tensor.transpose(turned[:, t, :], picked[:, t:PASS:PACK], ident[:])
                nc.vector.tensor_reduce(
                    target[:, PACK * g : PACK * (g + 1)], turned[:, :, first:P:PIECE_STEP], axis=X, op=ADD
                )

        kb_cols = tail.tile([P, PASSES * PACK], F32, name="kb_cols", align_bytes=64, offset=0)
        vs_wide = keep.tile([P, P], F32, name="vs_wide")
        nc.gpsimd.memset(vs_wide[:, PASSES * PACK : P], 0.0)

        gather_keys(0)
        columns(kb_row, KB_PART, kb_cols, 0, "kb")
        gather_keys(1)
        columns(vs_row, VS_PART, vs_wide, 2, "vs")
        vs_there = bank(4, [P, P], "vs_there")
        nc.tensor.transpose(vs_there[:], vs_wide[:], ident[:])
        vs_turned = keep.tile([P, P], F32, name="vs_turned")
        nc.scalar.copy(vs_turned[:], vs_there[:])
        vs_back = bank(7, [P, P], "vs_back")
        nc.tensor.transpose(vs_back[:], vs_turned[:], ident[:])
        gather_keys(2)

        q_first = k_first[:, :, 0:HALF, :]
        q_second = tail.tile([P, P, PACK], BF16, name="q_second", align_bytes=64, offset=20480)
        q_codes = keep.tile([P, QUERIES], U32, name="q_codes", align_bytes=64)
        q_scales = keep.tile([P, QUERIES], U8, name="q_scales", align_bytes=64)

        def quantize(codes, scales, source):
            nc.vector.quantize_mx(out=codes.bitcast(FP8X4), scales=scales, in_=source.rearrange("p x t -> p (x t)"))

        def quantize_queries(first, last, source):
            quantize(q_codes[:, first:last], q_scales[:, first:last], source)

        gather_keys(3)
        nc.vector.tensor_copy(
            q_first.rearrange("p h (c i) j -> p h c j i", i=RUN),
            q_raw[:, :, 0:P].rearrange("p j (h c i) -> p h c j i", h=2, i=RUN),
        )
        nc.scalar.copy(
            q_second[:].rearrange("p (c i) j -> p c j i", i=RUN),
            q_raw[:, :, P:QUERIES].rearrange("p j (c i) -> p c j i", i=RUN),
        )

        k_codes = [
            keep.tile([P, PASS], U32, name="k_codes0", align_bytes=64),
            tail.tile([P, PASS], U32, name="k_codes1", align_bytes=64, offset=20480),
        ]
        k_scales = keep.tile([P, SLOTS], U8, name="k_scales", align_bytes=64)

        def quantize_keys(g, t0, t1):
            first, last = PASS * g + P * t0, PASS * g + P * t1
            quantize(
                k_codes[g][:, P * t0 : P * t1],
                k_scales[:, first:last],
                k_packed[g][:, t0 // 2, t0 % 2 : t0 % 2 + t1 - t0, :, :].rearrange("p t m j -> p (t m) j"),
            )

        def score(index, g, t, q_cols):
            first, last = PASS * g + P * t, PASS * g + P * (t + 1)
            scores = bank(index % 7, [P, q_cols.stop - q_cols.start], "scores%d" % index)
            nc.tensor.matmul_mx(
                out=scores[:],
                lhsT=k_codes[g][:, P * t : P * (t + 1)].bitcast(FP8X4),
                lhsT_scale=k_scales[:, first:last],
                rhs=q_codes[:, q_cols].bitcast(FP8X4),
                rhs_scale=q_scales[:, q_cols],
                start=True,
                stop=True,
            )
            return scores[:]

        quantize_keys(0, 0, 1)
        for h in range(2):
            quantize_queries(HALF * h, HALF * (h + 1), q_first[:, h, :, :])
        quantize_keys(0, 1, 2)
        quantize_keys(0, 2, 4)
        quantize_queries(P, QUERIES, q_second[:])
        quantize_keys(1, 0, 2)
        quantize_keys(1, 2, 4)

        p_first = [keep.tile([P, PACK, P], F32, name="p_first%d" % b) for b in range(Q_BLOCKS)]
        p_last = tail.tile([P, PACK, QUERIES], F32, name="p_last", align_bytes=64, offset=12288)
        for b in range(Q_BLOCKS):
            for t in range(PACK):
                scores = score(PACK * b + t, 0, t, slice(P * b, P * (b + 1)))
                nc.scalar.activation(p_first[b][:, t, :], scores, SILU, bias=kb_cols[:, t : t + 1])
        for t in range(PACK):
            scores = score(2 * PACK + t, 1, t, slice(0, QUERIES))
            nc.scalar.activation(p_last[:, t, :], scores, SILU, bias=kb_cols[:, PACK + t : PACK + t + 1])

        around = keep.tile([P, 2, PASS // 2 + (QUERIES - SHARE) * PACK], BF16, name="around", align_bytes=64)
        v_second = keep.tile([P, 2, PASS // 2], BF16, name="v_second", align_bytes=64)
        v_picked = [around[:, :, 0 : PASS // 2], v_second[:]]
        w_first = keep.tile([P, QUERIES, PACK], BF16, name="w_first", align_bytes=64)
        w_own = around[:, 0, PASS // 2 :].rearrange("p (q t) -> p q t", t=PACK)
        w_shared = keep.tile([P, SHARE, PACK], BF16, name="w_shared", align_bytes=64)

        def weigh(engine, g, target, source, scales):
            width = target.shape[1]
            engine.tensor_tensor(
                target.rearrange("p (c i) t -> p c t i", i=RUN),
                source.rearrange("p t (c i) -> p c t i", i=RUN),
                scales[:, PACK * g : PACK * (g + 1)].unsqueeze(1).unsqueeze(3).to_broadcast([P, width // RUN, PACK, RUN]),
                MULT,
            )

        v_packed = [keep.tile([P, V_FEATURES, PACK], BF16, name="v_packed%d" % g, align_bytes=64) for g in range(PASSES)]

        def turn_values(g):
            turned = bank(5 + g, [P, 2, P], "v_turned%d" % g)
            for u in range(2):
                nc.tensor.transpose(turned[:, u, :], v_picked[g][:, u, :].bitcast(F32), ident[:])
            nc.scalar.copy(
                v_packed[g][:].rearrange("p e t -> p (e t)").bitcast(F32).rearrange("p (e u) -> p e u", u=2),
                turned[:].rearrange("p u e -> p e u"),
            )

        w_codes = [
            [
                keep.tile([P, P], U32, name="w_codes00", align_bytes=64),
                tail.tile([P, P], U32, name="w_codes01", align_bytes=64, offset=13312),
            ],
            [
                tail.tile([P, P], U32, name="w_codes10", align_bytes=64, offset=12288),
                tail.tile([P, P], U32, name="w_codes11", align_bytes=64, offset=12800),
            ],
        ]
        v_codes = [
            tail.tile([P, V_FEATURES], U32, name="v_codes%d" % g, align_bytes=64, offset=14336 + 512 * g)
            for g in range(PASSES)
        ]
        w_scales = keep.tile([P, PASSES, QUERIES], U8, name="w_scales", align_bytes=64)
        v_scales = keep.tile([P, PASSES, V_FEATURES], U8, name="v_scales", align_bytes=64)

        own = slice(0, QUERIES - SHARE)
        shared = slice(QUERIES - SHARE, QUERIES)
        for b in range(Q_BLOCKS):
            weigh(nc.vector, 0, w_first[:, P * b : P * (b + 1), :], p_first[b][:], vs_back)
        quantize(w_codes[0][0][:], w_scales[:, 0, 0:P], w_first[:, 0:P, :])
        weigh(nc.gpsimd, 1, w_shared[:], p_last[:, :, shared], vs_wide)
        for g in range(PASSES):
            gather(g, v_picked[g].rearrange("p u (m e) -> p m u e", e=2), v_pool)
        for g in range(PASSES):
            turn_values(g)
        weigh(nc.vector, 1, w_own, p_last[:, :, own], vs_back)
        quantize(w_codes[0][1][:], w_scales[:, 0, P:QUERIES], w_first[:, P:QUERIES, :])
        quantize(v_codes[0][:], v_scales[:, 0, :], v_packed[0][:])
        quantize(w_codes[1][0][:], w_scales[:, 1, 0:P], w_own[:, 0:P, :])
        quantize(v_codes[1][:], v_scales[:, 1, :], v_packed[1][:])
        quantize(w_codes[1][1][:], w_scales[:, 1, shared], w_shared[:])

        for b in range(Q_BLOCKS):
            q_cols = slice(P * b, P * (b + 1))
            y = bank(b, [P, V_FEATURES], "y%d" % b)
            for g in range(PASSES):
                nc.tensor.matmul_mx(
                    out=y[:],
                    lhsT=w_codes[g][b][:].bitcast(FP8X4),
                    lhsT_scale=w_scales[:, g, q_cols],
                    rhs=v_codes[g][:].bitcast(FP8X4),
                    rhs_scale=v_scales[:, g, :],
                    start=(g == 0),
                    stop=(g == PASSES - 1),
                )
            result = keep.tile([P, V_FEATURES], F32, name="result%d" % b)
            nc.vector.scalar_tensor_tensor(result[:], y[:], 1.0 / 16.0, gate[:, b, :], MULT, MULT)
            queue = nc.scalar if b == 0 else nc.sync
            queue.dma_start(out[0, q_cols, :], result[:])
